import numpy as np, ml_dtypes
CORES = [23,119,17,113]
N = 4
BF = ml_dtypes.bfloat16
NL, W, B, RO, Q = 112, 3584, 224, 8, 2
def parts(rng):
    X = rng.integers(0, 256, (N, 8, 16, W)); L = rng.integers(0, W, (N, 8, 16, W))
    y = (rng.integers(0, 256, (N, 8, 16, B)) * rng.integers(1, 9, (N, 8, 1, B))) >> 3
    return X, L, y, rng.integers(0, NL, (N, 8, B)), rng.integers(0, 4096, (N, 8, B))
def pack(X, L, y, ln, T):
    return {"xw": np.ascontiguousarray(X.reshape(N, 128, W)).astype(np.float32).astype(BF), "il": np.ascontiguousarray(L.reshape(N, 128, W)).astype(np.int32),
            "y0": np.ascontiguousarray(y.reshape(N, 128, B)).astype(np.float32).astype(BF), "ln0": np.ascontiguousarray(ln).astype(np.int32), "tk0": np.ascontiguousarray(T).astype(np.int32)}
def setup_inputs(rng):
    return pack(*parts(rng))
def setup_inputs_spread(rng):
    X = rng.integers(0, 256, (N, 8, 16, W)) >> rng.integers(0, 9, (N, 8, 1, W)); y = rng.integers(0, 256, (N, 8, 16, B)) >> rng.integers(0, 9, (N, 8, 1, B))
    a = np.exp2(rng.integers(-2, 3, (N, 8, 16, 1))); b = np.exp2(rng.integers(-2, 3, (N, 8, 16, 1)))
    line = np.minimum((NL * rng.random((N, 8, 16, W)) ** a).astype(np.int64), NL - 1); wait = np.minimum((32 * rng.random((N, 8, 16, W)) ** b).astype(np.int64), 31)
    ln = np.minimum((NL * rng.random((N, 8, B)) ** 3).astype(np.int64), NL - 1); T = np.minimum(np.exp2(12 * rng.random((N, 8, B))).astype(np.int64) - 1, 4095)
    return pack(X, 32 * line + wait, y, ln, T)
def ends(rng, top, *shape):
    k = rng.integers(0, 4, shape[:-2] + (1, shape[-1]))
    return top * np.where(k < 2, k, rng.integers(0, 2, shape))
def setup_inputs_ends(rng):
    X = ends(rng, 255, N, 8, 16, W); y = ends(rng, 255, N, 8, 16, B)
    L = np.where(rng.random((N, 8, 16, W)) < 0.8, ends(rng, W - 1, N, 8, 16, W), rng.integers(0, W, (N, 8, 16, W)))
    ln = (NL - 1) * rng.integers(0, 2, (N, 8, B)); T = 4095 * rng.integers(0, 2, (N, 8, B))
    L[..., 0] = 0; L[:, :, 1, 0] = W - 1; L[..., 31] = (W - 1) * rng.integers(0, 2, (N, 8, 16))
    L[..., W - 32] = W - 1; L[:, :, 0, W - 32] = 0; L[..., W - 1] = W - 1; L[:, :, 0, W - 1] = 0
    X[..., 0] = 0; X[..., W - 1] = 0; X[..., W - 2] = 255
    for q in range(N):
        if q == 1:
            for c in (0, 31, W - 2, W - 1): X[q, :, :, c] = 255
            y[q] = np.where(np.argsort(rng.random((8, 16, B)), axis=1) < rng.integers(0, 9, (8, 1, B)), 0, 255)
        else:
            if q == N - 1: y[q] = 0
            for i, l, t, v in ((0, NL - 1, 4095, 0), (B - 1, NL - 1, 4095, 0), (B - 2, NL - 1, 4095, 255), (1, NL - 1, 0, 255), (B - 4, NL - 1, 0, 255), (3, 0, 0, 0), (B - 3, 0, 0, 0)):
                ln[q, :, i] = l; T[q, :, i] = t; y[q, :, :, i] = v
            if q == N - 1: y[q, :7, :, B - 2] = 0
            if q == 2: y[q] = np.where(np.argsort(rng.random((8, 16, B)), axis=1) < rng.integers(9, 17, (8, 1, B)), 0, 255)
    return pack(X, L, y, ln, T)
def setup_inputs_corners(rng):
    X, L, y, ln, T = parts(rng)
    T = np.where(rng.random(T.shape) < 0.7, rng.choice(np.array([0, 15, 16, 31, 32, 4064, 4080, 4095]), T.shape), T)
    ln = np.where(rng.random(ln.shape) < 0.4, rng.choice(np.array([0, NL - 1]), ln.shape), ln)
    for q in range(N):
        for g in range(8):
            e = (q + g) % 8
            if e == 0: ln[q, g] = ln[q, g, 0]; T[q, g] = T[q, g, B - 1]
            elif e == 1: L[q, g] = np.arange(W)
            elif e == 2: L[q, g] = 0
            elif e == 3: L[q, g] = W - 1
            elif e == 4: X[q, g] = np.maximum(X[q, g], 1); y[q, g] = np.where(np.argsort(rng.random((16, B)), axis=0) < rng.integers(8, 10, (1, B)), 0, 255)
            elif e == 5: X[q, g] = 0
            elif e == 6: X[q, g] = 255; y[q, g] = rng.integers(128, 256, (16, B))
            else:
                a = rng.permutation(W)[:B]; ln[q, g] = a >> 5; T[q, g] = (a & 31) + 32 * rng.integers(0, 128, B); h = B // 4
                pl = np.concatenate([np.array([0, W - 1]), 1 + rng.permutation(W - 2)])
                d = rng.permutation(np.concatenate([pl[:h], pl[:h], pl[h:B - h]]))
                L[q, g, 15, a] = (d & 4064) + ((d - T[q, g]) & 31)
    return pack(X, L, y, ln, T)
def setup_inputs_crowd(rng):
    X, L, y, ln, T = parts(rng)
    few = rng.integers(0, NL, (N, 8, 1, 4)); few[:, ::2, :, 0] = NL - 1; few[:, 1::2, :, 1] = 0
    L[:, :, 0:2] = (L[:, :, 0:2] & 31) + 32 * np.take_along_axis(few, rng.integers(0, 4, (N, 8, 1, 2 * W)), 3).reshape(N, 8, 2, W)
    L[:, :, 15:16] = (L[:, :, 15:16] & 31) + 32 * np.take_along_axis(few, rng.integers(0, 2, (N, 8, 1, W)), 3)
    ln = np.take_along_axis(few, rng.integers(0, 4, (N, 8, 1, B)), 3).reshape(N, 8, B)
    p = int(rng.integers(0, N)); q = (p + 1) % N
    X[p] = 0; y[p] = 255 - (rng.integers(0, 128, (8, 16, B)) >> (3 * rng.integers(0, 2, (8, 1, B))))
    X[q] = np.maximum(X[q], 1); y[q] = rng.integers(128, 256, (8, 16, B))
    y[q, int(rng.integers(0, 8)), :, rng.permutation(B)[:int(rng.integers(1, 32))]] = 0
    return pack(X, L, y, ln, T)
def check_inputs(d):
    bad = []
    for k, hi in (("xw", 255), ("il", W - 1), ("y0", 255), ("ln0", NL - 1), ("tk0", 4095)):
        v = np.asarray(d[k]).astype(np.float64)
        if not np.all((v >= 0) & (v <= hi)): bad.append("range of " + k)
        elif not np.all(v == np.floor(v)): bad.append("whole numbers of " + k)
    return bad
def reference(xw, il, y0, ln0, tk0):
    X = xw.astype(np.float32).astype(np.int64).reshape(N, 8, 16, W); L = il.astype(np.int64).reshape(N, 8, 16, W)
    y = y0.astype(np.float32).astype(np.int64).reshape(N, 8, 16, B); ln = ln0.astype(np.int64); T = tk0.astype(np.int64)
    A = np.zeros(N, np.int64)
    for step in range(RO):
        a = 32 * ln + (T & 31)
        c = np.take_along_axis(L, a[:, :, None, :], 3)
        s = (c & 4064) + ((c + T[:, :, None, :]) & 31)
        v = np.take_along_axis(X, np.ascontiguousarray(s.transpose(0, 1, 3, 2)).reshape(N, 8, 1, 16 * B), 3).reshape(N, 8, 16, B, 16 // Q, Q)
        m = np.max(np.min(v, axis=-1), axis=-1)
        z = np.abs(m - y)
        skip = np.add.reduce((z >= y).astype(np.int64), axis=2) >= 9
        ln = np.where(skip, c[:, :, 1], c[:, :, 0]) >> 5
        d = s[:, :, 15]
        T = (T + 1 + (np.add.reduce(z, axis=2) & 31) + (A & 31)[:, None, None]) & 4095
        A = np.add.reduce(skip.reshape(N, 8 * B).astype(np.int64), axis=1)
        y = np.roll(z, 1, axis=0); ln = np.roll(ln, 1, axis=0); T = np.roll(T, 1, axis=0); d = np.roll(d, 1, axis=0)
        for q in range(N):
            for g in range(8):
                p, first = np.unique(d[q, g], return_index=True)
                u = L[q, g]; o = u[:, p]
                u[:, p] = (o & 4064) + ((o + y[q, g][:, first]) & 31)
        if step < RO - 1:
            np.put_along_axis(X, (16 * np.arange(B) + (T & 15))[:, :, None, :], y, 3)
    return {"yw": (L & 31).reshape(N, 128, W).astype(np.float32).astype(BF), "yy": y.reshape(N, 128, B).astype(np.float32).astype(BF), "yl": ln.astype(np.float32), "yt": T.astype(np.float32)}

@@ -1,0 +1,454 @@
+from concourse.mybir import AluOpType as A, AxisListType, ActivationFunctionType as AF
+
+NP, NB, NR, ST = 3584, 224, 4, 8
+CH = [(0, 10), (10, 24), (24, 42), (42, 64), (64, 92), (92, 112)]
+
+
+def _sb(dtype, **widths):
+    return {n: ("sbuf", [128, w], dtype) for n, w in widths.items()}
+
+
+SCRATCH = {
+    **_sb("int32", ilb=NP, TLi=2 * NB, TLj=2 * NB, iw=14, ip=14, ipq=14, SI=28, SJ=28, q=14, c2=28, b2=28, ao=28,
+          t1=14, t2=14, t3=14, Tn=14, Ai=1, Aj=1, B1=14, bwi=14),
+    **_sb("float16", f16t=NP, PM32=512, EF=8 * 240, EL=8 * 240, KQ=NB, fo=28),
+    **_sb("uint16", EO=8 * 240, DR=NB, DWu=16, OFF=16, AO=28),
+    **_sb("float32", h64=64, h32=32, rm=16, rq=16, wq1=1, th16=16, DG=NB, thA=NB, thB=NB, thr=NB, trash=14, DW=14,
+          o1=14, o2=14, dL=14, ldel=14, Ar=1, Af=1, fr=2 * NB),
+    **_sb("bfloat16", XT=NP, LT=NP, WT=NP + NB, YW=NP, KF=NP, TLb=3 * NB, ONE=128, ZER=128, BO0=128, BO=128, BOE=256,
+          ID=128, NID=128, NID32=128, P4=512, P32=512, SEL=2048, BC=2048, SKA=1024, SKD=1024, WQ=128, BIG=128,
+          MASK=1792, RST=NB, ZS=9 * 448, ZO=8 * NB, YE=8 * NB, LF=NB, SC=NB, DO=NB, KD=NB, DRED=NB, sel=14, bw=14,
+          BR=NB, WA=NB, LG=NB, VE=1792, U=1792, M=1792),
+    "EQ": ("sbuf", [128, 14, 240], "bfloat16"),
+    **{n: ("psum", [128, 512], "float32") for n in ("pXR", "pE", "pO", "pZ", "pW", "pS", "pD", "pC")},
+}
+SEMAPHORES = (["cv", "ct", "cs", "cp", "loc", "d_tk", "d_ln", "d_y", "d_x0", "d_x1", "d_t", "d_l"]
+              + ["d_il%d" % i for i in range(7)] + ["d_o%d" % i for i in range(8)]
+              + ["a%s%d" % (k, n) for k in "zye" for n in range(ST)])
+
+
+def rank_program(g, core, T, topo):
+    rank = T.rank_of(core)
+    if rank is None:
+        return
+    queues = {"v": g.vector, "t": g.tensor, "s": g.scalar, "p": g, "y": g.sync}
+    semof = {"v": "cv", "t": "ct", "s": "cs", "p": "cp"}
+    count = {s: 0 for s in SEMAPHORES}
+    known = {e: {} for e in queues}
+    snaps = {}
+    hist = {}
+
+    def conflicts(e, name, lo, hi, write):
+        bank = name[0] == "p" and name[1:2].isupper()
+        out = []
+        for (a, b, e2, s2, v2, w2, asy) in hist.get(name, []):
+            if bank:
+                if e2 == e:
+                    if e == "t" or not (write or w2) or b <= lo or hi <= a:
+                        continue
+                out.append((s2, v2))
+                continue
+            if b <= lo or hi <= a or not (write or w2):
+                continue
+            if e2 == e and not asy and not w2:
+                continue
+            out.append((s2, v2))
+        return out
+
+    def waits(e, acc):
+        need = {}
+        for (name, lo, hi, w) in acc:
+            for s, v in conflicts(e, name, lo, hi, w):
+                need[s] = max(need.get(s, 0), v)
+        own = semof.get(e)
+        for s in sorted(need, key=lambda s: (s == own, s)):
+            v = need[s]
+            if known[e].get(s, 0) >= v:
+                continue
+            queues[e].wait_ge(T.sem[s], v)
+            for s2, v2 in snaps[(s, v)].items():
+                known[e][s2] = max(known[e].get(s2, 0), v2)
+
+    def note(e, acc, s, v, asy):
+        sn = dict(known[e]) if e in known else {}
+        sn[s] = v
+        snaps[(s, v)] = sn
+        for (name, lo, hi, w) in acc:
+            h = hist.setdefault(name, [])
+            if w:
+                h[:] = [x for x in h if not (lo <= x[0] and x[1] <= hi)]
+            else:
+                h[:] = [x for x in h if not (x[2] == e and not x[5] and not asy and lo <= x[0] and x[1] <= hi)]
+            h.append((lo, hi, e, s, v, w, asy))
+
+    def access(rd, wr):
+        return [(n, lo, hi, False) for (n, lo, hi) in rd] + [(n, lo, hi, True) for (n, lo, hi) in wr]
+
+    def op(e, rd, wr, fn):
+        acc = access(rd, wr)
+        waits(e, acc)
+        s = semof[e]
+        count[s] += 1
+        fn(queues[e]).then_inc(T.sem[s], 1)
+        note(e, acc, s, count[s], False)
+
+    def dma(e, rd, wr, out, in_, s):
+        acc = access(rd, wr)
+        waits(e, acc)
+        count[s] += 16
+        queues[e].dma_start(out, in_).then_inc(T.sem[s], 16)
+        note(e, acc, s, count[s], True)
+
+    def ap(o):
+        if o[0] == "EQ":
+            c, a = divmod(o[1], 240)
+            return T.EQ[:, c, a:a + o[2] - o[1]] if len(o) == 3 else T.EQ[:, :, 0:16]
+        if len(o) == 1:
+            return T[o[0]][:]
+        if len(o) == 4:
+            return T[o[0]][:, o[1]:o[2]:o[3]]
+        return T[o[0]][:, o[1]:o[2]]
+
+    def rg(o):
+        return (o[0], 0, SCRATCH[o[0]][1][1]) if len(o) == 1 else (o[0], o[1], o[2])
+
+    def vts(out, i, s1, o0, s2=None, o1=None):
+        rd = [rg(i)]
+        if isinstance(s1, tuple):
+            rd.append(rg(s1))
+            s1 = ap(s1)
+        if o1 is None:
+            op("v", rd, [rg(out)], lambda q: q.tensor_scalar(ap(out), ap(i), s1, None, o0))
+        else:
+            op("v", rd, [rg(out)], lambda q: q.tensor_scalar(ap(out), ap(i), s1, s2, o0, o1))
+
+    def vtt(out, a, b, o):
+        op("v", [rg(a), rg(b)], [rg(out)], lambda q: q.tensor_tensor(ap(out), ap(a), ap(b), o))
+
+    def vcp(out, i):
+        op("v", [rg(i)], [rg(out)], lambda q: q.tensor_copy(ap(out), ap(i)))
+
+    def fill(out, c):
+        op("v", [], [rg(out)], lambda q: q.memset(ap(out), c))
+
+    def act(out, i, f, **kw):
+        op("s", [rg(i)] + ([("rm", 0, 16)] if "scale" in kw else []), [rg(out)], lambda q: q.activation(ap(out), ap(i), f, **kw))
+
+    def gat(out, win, off):
+        op("s", [rg(win), rg(off)], [rg(out)], lambda q: q.activation(ap(out), ap(win).indirect(ap(off)), AF.Copy))
+
+    def mm(out, l, r, start, stop):
+        op("t", [rg(l), rg(r)], [rg(out)], lambda q: q.matmul(ap(out), ap(l), ap(r), start, stop))
+
+    def mat(n, r):
+        return (n, 128 * r, 128 * r + 128)
+
+    nxt = T.cores[(rank + 1) % NR]
+    prv = T.cores[(rank - 1) % NR]
+    rid, pid = topo.addr(nxt)[:2]
+    emask = topo.mask(core, nxt)
+    n_out = len(topo.engines(core, nxt))
+    n_in = len(topo.engines(prv, core))
+
+    def send(dst, src, s):
+        waits("p", [rg(src) + (False,)])
+        g.remote_dma(out_ap=ap(dst), in_ap=ap(src), remote_sem=T.sem[s], local_sem=T.sem["loc"], pid=pid,
+                     routing_id=rid, dma_engine_mask=emask)
+        count["loc"] += n_out
+
+    def lands(dst, s):
+        count[s] = n_in
+        note("r", [rg(dst) + (True,)], s, n_in, True)
+
+    def zin(n):
+        return ("ZS", 448 * n, 448 * n + 224)
+
+    def ye(n):
+        return ("YE", 224 * n, 224 * n + 224)
+
+    def lst(n, b, lo, hi):
+        return (b, 240 * n + lo, 240 * n + hi)
+
+    for n in range(ST):
+        lands(ye(n), "ay%d" % n)
+        lands(lst(n, "EL", 0, 238), "ae%d" % n)
+        lands(zin(n + 1), "az%d" % n)
+
+    fill(("TLi",), 0)
+    fill(("ONE",), 1.0)
+    for i in range(7):
+        b = ("ilb", 512 * i, 512 * i + 512)
+        dma("y", [], [rg(b)], ap(b), T.il[:, 512 * i:512 * i + 512], "d_il%d" % i)
+    dma("s", [], [("TLi", 0, 224)], T.TLi[0:128:16, 0:224], T.tk0[:], "d_tk")
+    dma("s", [], [("TLi", 224, 448)], T.TLi[0:128:16, 224:448], T.ln0[:], "d_ln")
+    dma("s", [], [rg(zin(0))], ap(zin(0)), T.y0[:], "d_y")
+    for i in range(2):
+        b = ("XT", 1792 * i, 1792 * i + 1792)
+        dma("y", [], [rg(b)], ap(b), T.xw[:, 1792 * i:1792 * i + 1792], "d_x%d" % i)
+
+    def asel(out, i, pat, cmp, base, cm, other=0.0):
+        op("p", [rg(i)], [rg(out)], lambda q: q.affine_select(ap(out), ap(i), pat, cmp, other, base, cm))
+    asel(("BO0",), ("ONE",), [[-16, 8], [0, 16]], A.is_ge, 0, 1)
+    asel(("BO",), ("BO0",), [[16, 8], [0, 16]], A.is_ge, 15, -1)
+    asel(("ID",), ("ONE",), [[-1, 128]], A.is_equal, 0, 1)
+    asel(mat("BOE", 0), ("BO",), [[0, 8], [-1, 16]], A.is_ge, 7, 0)
+    asel(mat("BOE", 1), ("BO",), [[0, 8], [1, 16]], A.is_ge, -8, 0)
+    for k, (h, base) in enumerate(((0, 0), (1, 16), (0, -1), (1, 15))):
+        asel(mat("P4", k), mat("BOE", h), [[-16, 8], [-2, 16]], A.is_equal, base, 1)
+    op("p", [], [("iw", 0, 14)], lambda q: q.iota(T.iw[:], [[16, 14]], 0, 1))
+    op("p", [], [("ip", 0, 14)], lambda q: q.iota(T.ip[:], [[0, 14]], 0, 1))
+    fill(("SEL",), 0.0)
+    for r in range(16):
+        vcp(("SEL", 128 * r + r, 128 * r + 128, 16), ("BO", r, 128, 16))
+    vts(("NID32",), ("ID",), -32.0, A.mult)
+    for m in ("SKD", "SKA"):
+        asel((m,), ("SEL", 0, 1024), [[0, 1024]], A.is_ge, -1, 0)
+    asel(("ZER",), ("ID",), [[0, 128]], A.is_ge, -1, 0)
+    for k in range(2):
+        asel(("MASK", 896 * k, 896 * k + 896), ("SKA", 0, 896), [[0, 112], [1, 8]], A.is_equal, 0, 0, 256.0)
+    asel(("RST",), ("SKA", 0, 224), [[0, 14], [1, 16]], A.is_equal, 0, 0, 1.0)
+
+    def table(i):
+        lo, hi = 512 * i, 512 * i + 512
+        vts(("f16t", lo, hi), ("ilb", lo, hi), -1792.0, A.add)
+        vts(("LT", lo, hi), ("f16t", lo, hi), 1.0 / 32, A.mult, 184.515625, A.add)
+        pb = ("pXR", "pE", "pO", "pZ")[i % 4]
+        mm((pb,), ("ID",), ("f16t", lo, hi), True, False)
+        mm((pb,), ("NID32",), ("LT", lo, hi), False, True)
+        act(("WT", lo, hi), (pb,), AF.Copy, bias=5920.0)
+
+    def clocks():
+        vts(("TLj", 0, 224), ("TLi", 0, 224), 4064, A.bitwise_and)
+        vts(("TLj", 224, 448), ("TLi", 0, 224), 31, A.bitwise_and)
+        vcp(("TLb", 0, 448), ("TLj",))
+        vcp(("TLb", 448, 672), ("TLi", 224, 448))
+        for r in range(16):
+            mm(("pW", 0, 42), mat("SEL", r), ("TLb", r, 672, 16), r == 0, r == 15)
+
+    def places():
+        vcp(("c2", 0, 14), ("pW", 14, 28))
+        vcp(("bw",), ("pW", 14, 28))
+        vts(("b2", 0, 14), ("pW", 28, 42), 32.0, A.mult)
+        vcp(("t1",), ("pW", 0, 14))
+        vtt(("ao", 0, 14), ("c2", 0, 14), ("b2", 0, 14), A.add)
+        vcp(("AO", 0, 14), ("ao", 0, 14))
+        vtt(("Tn",), ("t1",), ("c2", 0, 14), A.add)
+
+    def broadcast(dst, src, lo):
+        for r in range(16):
+            mm((dst, r + lo, lo + 224, 16), mat("BC", r), src, True, True)
+
+    def pick(m, k):
+        for t in range(8):
+            for h in range(2):
+                act((m, 128 * t + 2 * t + h, 128 * t + 128, 16), ("ID", k + 8 * h, 128, 16), AF.Copy)
+
+    def weights():
+        for r in range(16):
+            fill(("th16", r, r + 1), 2.0 * 4.0 ** (15 - r))
+        vtt(("rq",), ("rm",), ("th16",), A.mult)
+        op("v", [("rq", 0, 16)], [("wq1", 0, 1)], lambda q: q.tensor_reduce(T.wq1[:], T.rq[:], AxisListType.X, A.add))
+        vts(("WQ",), ("BO",), ("wq1", 0, 1), A.mult, 0.5, A.mult)
+        vts(("BIG",), ("BO",), 2.0 ** 32, A.mult)
+        vcp(("DG", 0, 16), ("rm",))
+        for a, b in ((16, 16), (32, 32), (64, 64), (128, 96)):
+            vcp(("DG", a, a + b), ("DG", 0, b))
+        vts(("thA",), ("DG",), ("wq1", 0, 1), A.mult)
+        vts(("thB",), ("DG",), -1e29, A.mult, 1e29, A.add)
+        vtt(("thr",), ("thA",), ("thB",), A.add)
+        vts(("ipq",), ("ip",), 112, A.bitwise_and)
+        vtt(("iw",), ("iw",), ("ipq",), A.subtract)
+        vts(("b2", 14, 28), ("iw",), 16.0, A.mult)
+        vts(("trash",), ("iw",), 3584.0, A.add)
+
+    table(0)
+    vtt(("h64",), ("ID", 0, 64), ("ID", 64, 128), A.add)
+    vtt(("h32",), ("h64", 0, 32), ("h64", 32, 64), A.add)
+    vtt(("rm",), ("h32", 0, 16), ("h32", 16, 32), A.add)
+    table(1)
+    for r in range(16):
+        act(mat("BC", r), ("BO",), AF.Copy, scale=T.rm[:, r:r + 1])
+    table(2)
+    table(3)
+    clocks()
+    table(4)
+    pick("SKD", 7)
+    places()
+    table(5)
+    table(6)
+    broadcast("pS", ("bw",), 256)
+    act(("BR",), ("pS", 256, 480), AF.Copy)
+    vts(("PM32",), ("P4",), -32.0, A.mult)
+    vts(("P32",), ("P4",), 32.0, A.mult)
+    vts(("NID",), ("ID",), -1.0, A.mult)
+    weights()
+
+    def rewrite(z):
+        op("v", [rg(z), ("DRED", 0, 224), ("OFF", 0, 14)], [("WT", 0, NP + NB)],
+           lambda q: q.tensor_tensor(T.WT[:, 0:NP + NB].indirect(T.OFF[:, 0:14]), T.DRED[:], ap(z), A.add))
+
+    def arrive(n):
+        z = zin(n)
+        vtt(("ZS", 448 * n + 224, 448 * n + 448), z, ("pD", 256, 480), A.is_ge)
+        if n < ST:
+            mm(("pXR", 0, 224), ("BO",), z, True, False)
+        for r in range(16):
+            mm(("pW", 0, 28), mat("SEL", r), ("ZS", 448 * n + r, 448 * n + 448, 16), r == 0, r == 15)
+        if n < ST:
+            rewrite(z)
+        vts(("sel",), ("pW", 14, 28), 9.0, A.is_ge)
+        vtt(("q",), ("pW", 0, 14), ("B1",), A.add)
+        vtt(("ldel",), ("sel",), ("dL",), A.mult)
+        if n < ST:
+            vts(("c2", 0, 14), ("q",), 31, A.bitwise_and)
+            vtt(("b2", 0, 14), ("ldel",), ("SJ", 0, 14), A.add)
+            vts(("c2", 14, 28), ("q",), 15, A.bitwise_and)
+            vtt(("ao",), ("c2",), ("b2",), A.add)
+            vcp(("AO",), ("ao",))
+            op("v", [rg(z), ("AO", 14, 28)], [("XT", 0, NP)],
+               lambda q: q.tensor_copy(T.XT[:, 0:NP].indirect(T.AO[:, 14:28]), ap(z)))
+
+    def clock():
+        vcp(("t1",), ("pW", 0, 14))
+        vts(("t2",), ("t1",), 31, A.bitwise_and)
+        vtt(("t3",), ("t2",), ("B1",), A.add)
+        vts(("Tn",), ("t3",), 4095, A.bitwise_and)
+
+    def fetch(n):
+        gat(("WA",), ("WT", 0, NP), ("AO", 0, 14))
+        gat(("LG",), ("LT", 0, NP), ("AO", 0, 14))
+        mm(("pXR", 0, 224), ("ID",), ("BR",), n == 0, False)
+        for k, b in ((0, "pE"), (2, "pO")):
+            o = (b, 0, 112)
+            for h in range(2):
+                mm(o, mat("P4", k + h), ("BR", h, 224, 2), h == 0, False)
+            if n:
+                for h in range(2):
+                    mm(o, mat("BOE", h), ("ZS", 448 * n + h, 448 * n + 224, 2), False, False)
+        mm(("pXR", 0, 224), ("ID",), ("WA",), False, True)
+        vts(("KQ",), ("pXR", 0, 224), 1.0 / 32, A.mult, 1535.515625, A.add)
+        if n:
+            clock()
+        vts(lst(n, "EF", 224, 238), ("Tn",), -2048.0, A.add)
+        for k, b, srcs in ((0, "pE", ("WA", "LG", "KQ")), (2, "pO", ("WA", "LG", "KQ"))):
+            for src in srcs:
+                for h in range(2):
+                    mm((b, 0, 112), mat({"WA": "P4", "LG": "P32", "KQ": "PM32"}[src], k + h), (src, h, 224, 2),
+                       False, src == "KQ" and h == 1)
+        vts(lst(n, "EO", 0, 112), ("pE", 0, 112), 45024.0, A.add)
+        vts(lst(n, "EO", 112, 224), ("pO", 0, 112), 45024.0, A.add)
+        vts(lst(n, "EF", 0, 224), lst(n, "EO", 0, 224), -1792.0, A.add)
+
+    def big(n):
+        for (a, b) in CH:
+            gat(("VE", 16 * a, 16 * b), ("XT", 0, NP), lst(n, "EO", a, b))
+        mm(("pZ", 0, 224), ("NID",), zin(n), True, False)
+
+        def least(a, b):
+            off = lst(n, "EO", 112 + a, 112 + b)
+            op("v", [("XT", 0, NP), rg(off), ("VE", 16 * a, 16 * b)], [("U", 16 * a, 16 * b)],
+               lambda q: q.tensor_tensor(T.U[:, 16 * a:16 * b], T.XT[:, 0:NP].indirect(ap(off)), T.VE[:, 16 * a:16 * b], A.min))
+
+        def greatest(a, b):
+            r = slice(16 * a, 16 * b)
+            op("v", [("MASK", 16 * a, 16 * b), ("U", 16 * a, 16 * b)], [("M", 16 * a, 16 * b)],
+               lambda q: q.tensor_tensor_scan(T.M[:, r], T.MASK[:, r], T.U[:, r], 0.0, A.min, A.max))
+            mm(("pZ", 2 * a, 2 * b), ("ID",), ("M", 16 * a + 7, 16 * b, 8), False, b == 112)
+        for c in CH:
+            least(*c)
+            greatest(*c)
+        act(("ZO", 224 * n, 224 * n + 224), ("pZ", 0, 224), AF.Abs)
+
+    def ready(n):
+        el = 240 * n
+        for k in (7, 15):
+            mm(("pD", k // 8, 224, 2), mat("BC", k), ("EL", el + 112, el + 224), True, True)
+        for t in range(8):
+            mm(("pD", 224, 238), mat("SKD", t), ("EL", el + 112 + t, el + 224, 8), t == 0, t == 7)
+        if n == 0:
+            pick("SKA", 0)
+        for t in range(8):
+            mm(("pS", 0, 28), mat("SKA", t), ("EL", el + t, el + 224, 8), t == 0, t == 7)
+        if n:
+            op("v", [("pW", 32, 46)], [("Ar", 0, 1)], lambda q: q.tensor_reduce(T.Ar[:], T.pW[:, 32:46], AxisListType.X, A.add))
+            vcp(("Ai",), ("Ar",))
+            vts(("Aj",), ("Ai",), 31, A.bitwise_and)
+            vcp(("Af",), ("Aj",))
+            vts(("B1",), lst(n, "EL", 224, 238), ("Af", 0, 1), A.add, 2049.0, A.add)
+        else:
+            vts(("B1",), lst(n, "EL", 224, 238), 2049.0, A.add)
+        vts(("DW",), ("pD", 224, 238), 1792.0, A.add)
+        vts(("DR",), ("pD", 0, 224), 1792.0, A.add)
+        vcp(("DWu", 0, 14), ("DW",))
+        gat(("DO",), ("WT", 0, NP), ("DWu", 0, 14))
+        mm(("pC", 0, 224), ("ZER",), ("MASK", 0, 224), True, False)
+        for c in range(14):
+            e = ("EQ", 240 * c, 240 * c + 224 - 16 * c)
+            vts(e, ("DR", 16 * c, 224), ("DW", c, c + 1), A.is_equal)
+            if c < 13:
+                mm(("pC", 16 * c + 16, 224), ("BIG",), (e[0], e[1] + 16, e[2]), False, False)
+            if c == 7:
+                vts(("bwi",), ("B1",), 31, A.bitwise_and)
+                vcp(("bw",), ("bwi",))
+        mm(("pC", 0, 224), ("WQ",), ("EQ", 0, 14 * 240, 1), False, True)
+        vts(("KD",), ("DO",), 1.0 / 32, A.mult, 191.515625, A.add)
+        mm(("pZ", 0, 224), ("ID",), ("DO",), True, False)
+        mm(("pZ", 0, 224), ("NID32",), ("KD",), False, True)
+        act(("DRED",), ("pZ", 0, 224), AF.Copy, bias=5984.0)
+        mm(("pD", 256, 480), ("ID",), ye(n), True, True)
+        vtt(("LF",), ("pC", 0, 224), ("thr",), A.is_gt)
+        op("v", [("RST", 0, 224), ("LF", 0, 224)], [("SC", 0, 224)],
+           lambda q: q.tensor_tensor_scan(T.SC[:], T.RST[:], T.LF[:], 0.0, A.mult, A.add))
+        vtt(("o1",), ("SC", 15, 224, 16), ("trash",), A.mult)
+        vtt(("o2",), ("o1",), ("DW",), A.max)
+        vcp(("OFF", 0, 14), ("o2",))
+        vts(("SI",), ("pS", 0, 28), 1792.0, A.add)
+        vts(("SJ",), ("SI",), 4064, A.bitwise_and)
+        vtt(("dL",), ("SJ", 14, 28), ("SJ", 0, 14), A.subtract)
+        if n < ST - 1:
+            broadcast("pS", ("bw",), 256)
+            act(("BR",), ("pS", 256, 480), AF.Copy)
+
+    for n in range(ST):
+        if n:
+            arrive(n)
+        send(ye(n), zin(n), "ay%d" % n)
+        fetch(n)
+        if n:
+            mm(("pW", 32, 46), ("ONE",), ("sel",), True, True)
+        send(lst(n, "EL", 0, 238), lst(n, "EF", 0, 238), "ae%d" % n)
+        big(n)
+        send(zin(n + 1), ("ZO", 224 * n, 224 * n + 224), "az%d" % n)
+        ready(n)
+
+    dma("y", [rg(zin(ST))], [], T.yy[:], ap(zin(ST)), "d_o0")
+    rewrite(zin(ST))
+    arrive(ST)
+    for i in range(7):
+        lo, hi = 512 * i, 512 * i + 512
+        vts(("KF", lo, hi), ("WT", lo, hi), 1.0 / 32, A.mult, 191.515625, A.add)
+        if i == 1:
+            clock()
+            vts(("fo", 0, 14), ("Tn",), -2048.0, A.add)
+            vtt(("fo", 14, 28), ("ldel",), ("SJ", 0, 14), A.add)
+            for r in range(16):
+                mm(("pS", r, 448, 16), mat("BC", r), ("fo",), True, True)
+        if i in (3, 6):
+            vts(("f16t", lo, hi), ("KF", lo, hi), -32.0, A.mult, 6144.0, A.add)
+            vtt(("YW", lo, hi), ("WT", lo, hi), ("f16t", lo, hi), A.add)
+        else:
+            pb = ("pE", "pO", "pZ")[i % 3]
+            mm((pb,), ("ID",), ("WT", lo, hi), True, False)
+            mm((pb,), ("NID32",), ("KF", lo, hi), False, True)
+            act(("YW", lo, hi), (pb,), AF.Copy, bias=6144.0)
+        if i == 3:
+            vts(("fr", 0, 224), ("pS", 0, 224), 2048.0, A.add)
+            vts(("fr", 224, 448), ("pS", 224, 448), 1.0 / 32, A.mult)
+            dma("y", [("fr", 0, 224)], [], T.yt[:], T.fr[0:128:16, 0:224], "d_t")
+            dma("y", [("fr", 224, 448)], [], T.yl[:], T.fr[0:128:16, 224:448], "d_l")
+    for i in range(7):
+        lo, hi = 512 * i, 512 * i + 512
+        dma("y", [("YW", lo, hi)], [], T.yw[:, lo:hi], T.YW[:, lo:hi], "d_o%d" % (1 + i))
+    for s in SEMAPHORES:
+        if count[s] and known["p"].get(s, 0) < count[s]:
+            g.wait_ge(T.sem[s], count[s])

@@ -1,7 +1,8 @@
 from concourse.mybir import AluOpType as A, AxisListType, ActivationFunctionType as AF
 
 NP, NB, NR, ST = 3584, 224, 4, 8
-CH = [(0, 10), (10, 24), (24, 42), (42, 64), (64, 92), (92, 112)]
+RB = 3
+CH = [(0, 14), (14, 30), (30, 50), (50, 74), (74, 98), (98, 112)]
 
 
 def _sb(dtype, **widths):
@@ -10,14 +11,14 @@ def _sb(dtype, **widths):
 
 SCRATCH = {
     **_sb("int32", ilb=NP, TLi=2 * NB, TLj=2 * NB, iw=14, ip=14, ipq=14, SI=28, SJ=28, q=14, c2=28, b2=28, ao=28,
-          t1=14, t2=14, t3=14, Tn=14, Ai=1, Aj=1, B1=14, bwi=14),
+          t1=14, t2=14, t3=14, Tn=14, B1=14),
     **_sb("float16", f16t=NP, PM32=512, EF=8 * 240, EL=8 * 240, KQ=NB, fo=28),
     **_sb("uint16", EO=8 * 240, DR=NB, DWu=16, OFF=16, AO=28),
-    **_sb("float32", h64=64, h32=32, rm=16, rq=16, wq1=1, th16=16, DG=NB, thA=NB, thB=NB, thr=NB, trash=14, DW=14,
-          o1=14, o2=14, dL=14, ldel=14, Ar=1, Af=1, fr=2 * NB),
+    **_sb("float32", h64=64, h32=32, rm=16, rq=16, wq1=1, th16=16, DG=NB, thA=NB, thB=NB, thr=NB, trm=NB, SC=NB, DW=14,
+          o2=14, sd=28, sa=28, lin=28, Ar=1, Au=1, A1=1, fr=2 * NB),
     **_sb("bfloat16", XT=NP, LT=NP, WT=NP + NB, YW=NP, KF=NP, TLb=3 * NB, ONE=128, ZER=128, BO0=128, BO=128, BOE=256,
           ID=128, NID=128, NID32=128, P4=512, P32=512, SEL=2048, BC=2048, SKA=1024, SKD=1024, WQ=128, BIG=128,
-          MASK=1792, RST=NB, ZS=9 * 448, ZO=8 * NB, YE=8 * NB, LF=NB, SC=NB, DO=NB, KD=NB, DRED=NB, sel=14, bw=14,
+          MASK=1792, ZS=9 * 448, ZO=8 * NB, YE=8 * 448, LF=NB, KA=1, DO=NB, KD=NB, DRED=NB, sel=14, bw=14,
           BR=NB, WA=NB, LG=NB, VE=1792, U=1792, M=1792),
     "EQ": ("sbuf", [128, 14, 240], "bfloat16"),
     **{n: ("psum", [128, 512], "float32") for n in ("pXR", "pE", "pO", "pZ", "pW", "pS", "pD", "pC")},
@@ -117,6 +118,9 @@ def rank_program(g, core, T, topo):
         if isinstance(s1, tuple):
             rd.append(rg(s1))
             s1 = ap(s1)
+        if isinstance(s2, tuple):
+            rd.append(rg(s2))
+            s2 = ap(s2)
         if o1 is None:
             op("v", rd, [rg(out)], lambda q: q.tensor_scalar(ap(out), ap(i), s1, None, o0))
         else:
@@ -164,13 +168,16 @@ def rank_program(g, core, T, topo):
         return ("ZS", 448 * n, 448 * n + 224)
 
     def ye(n):
-        return ("YE", 224 * n, 224 * n + 224)
+        return ("YE", 448 * n, 448 * n + 224)
+
+    def row(n):
+        return ("ZS", 448 * n + 224, 448 * n + 448)
 
     def lst(n, b, lo, hi):
         return (b, 240 * n + lo, 240 * n + hi)
 
     for n in range(ST):
-        lands(ye(n), "ay%d" % n)
+        lands(("YE", 448 * n, 448 * n + 448), "ay%d" % n)
         lands(lst(n, "EL", 0, 238), "ae%d" % n)
         lands(zin(n + 1), "az%d" % n)
 
@@ -206,7 +213,6 @@ def rank_program(g, core, T, topo):
     asel(("ZER",), ("ID",), [[0, 128]], A.is_ge, -1, 0)
     for k in range(2):
         asel(("MASK", 896 * k, 896 * k + 896), ("SKA", 0, 896), [[0, 112], [1, 8]], A.is_equal, 0, 0, 256.0)
-    asel(("RST",), ("SKA", 0, 224), [[0, 14], [1, 16]], A.is_equal, 0, 0, 1.0)
 
     def table(i):
         lo, hi = 512 * i, 512 * i + 512
@@ -254,12 +260,14 @@ def rank_program(g, core, T, topo):
         for a, b in ((16, 16), (32, 32), (64, 64), (128, 96)):
             vcp(("DG", a, a + b), ("DG", 0, b))
         vts(("thA",), ("DG",), ("wq1", 0, 1), A.mult)
-        vts(("thB",), ("DG",), -1e29, A.mult, 1e29, A.add)
+        vts(("thB",), ("DG",), 1.0, A.subtract)
         vtt(("thr",), ("thA",), ("thB",), A.add)
         vts(("ipq",), ("ip",), 112, A.bitwise_and)
         vtt(("iw",), ("iw",), ("ipq",), A.subtract)
         vts(("b2", 14, 28), ("iw",), 16.0, A.mult)
-        vts(("trash",), ("iw",), 3584.0, A.add)
+        op("p", [], [("trm", 0, 224)], lambda q: q.iota(T.trm[:], [[1, 224]], NP, 0, allow_small_or_imprecise_dtypes=True))
+        vtt(("trm",), ("trm",), ("DG",), A.mult)
+        fill(("sd",), 0.0)
 
     table(0)
     vtt(("h64",), ("ID", 0, 64), ("ID", 64, 128), A.add)
@@ -277,15 +285,11 @@ def rank_program(g, core, T, topo):
     table(5)
     table(6)
     broadcast("pS", ("bw",), 256)
-    act(("BR",), ("pS", 256, 480), AF.Copy)
+    act(row(0), ("pS", 256, 480), AF.Copy)
     vts(("PM32",), ("P4",), -32.0, A.mult)
     vts(("P32",), ("P4",), 32.0, A.mult)
     vts(("NID",), ("ID",), -1.0, A.mult)
     weights()
-
-    def rewrite(z):
-        op("v", [rg(z), ("DRED", 0, 224), ("OFF", 0, 14)], [("WT", 0, NP + NB)],
-           lambda q: q.tensor_tensor(T.WT[:, 0:NP + NB].indirect(T.OFF[:, 0:14]), T.DRED[:], ap(z), A.add))
 
     def arrive(n):
         z = zin(n)
@@ -294,55 +298,68 @@ def rank_program(g, core, T, topo):
             mm(("pXR", 0, 224), ("BO",), z, True, False)
         for r in range(16):
             mm(("pW", 0, 28), mat("SEL", r), ("ZS", 448 * n + r, 448 * n + 448, 16), r == 0, r == 15)
-        if n < ST:
-            rewrite(z)
-        vts(("sel",), ("pW", 14, 28), 9.0, A.is_ge)
+        vtt(("o2",), ("SC", 15, 224, 16), ("DW",), A.max)
+        vts(("SI",), ("pS", 0, 28), 1792.0, A.add)
+        vcp(("OFF", 0, 14), ("o2",))
+        vts(("SJ",), ("SI",), 4064, A.bitwise_and)
+        op("v", [rg(z), ("DRED", 0, 224), ("OFF", 0, 14)], [("WT", 0, NP + NB)],
+           lambda q: q.tensor_tensor(T.WT[:, 0:NP + NB].indirect(T.OFF[:, 0:14]), T.DRED[:], ap(z), A.add))
+        vtt(("sd", 1, 28, 2), ("SJ", 14, 28), ("SJ", 0, 14), A.subtract)
+        vcp(("sa", 1, 28, 2), ("SJ", 0, 14))
         vtt(("q",), ("pW", 0, 14), ("B1",), A.add)
-        vtt(("ldel",), ("sel",), ("dL",), A.mult)
+        vts(("sa", 0, 28, 2), ("pW", 14, 28), 9.0, A.is_ge)
+        vcp(("t1",), ("pW", 0, 14))
         if n < ST:
             vts(("c2", 0, 14), ("q",), 31, A.bitwise_and)
-            vtt(("b2", 0, 14), ("ldel",), ("SJ", 0, 14), A.add)
             vts(("c2", 14, 28), ("q",), 15, A.bitwise_and)
-            vtt(("ao",), ("c2",), ("b2",), A.add)
+        op("v", [("sd", 0, 28), ("sa", 0, 28)], [("lin", 0, 28)],
+           lambda q: q.tensor_tensor_scan(T.lin[:], T.sd[:], T.sa[:], 0.0, A.mult, A.add))
+        vts(("t2",), ("t1",), 31, A.bitwise_and)
+        if n < ST:
+            vtt(("ao", 14, 28), ("c2", 14, 28), ("b2", 14, 28), A.add)
+            vtt(("ao", 0, 14), ("c2", 0, 14), ("lin", 1, 28, 2), A.add)
+        vtt(("t3",), ("t2",), ("B1",), A.add)
+        if n < ST:
             vcp(("AO",), ("ao",))
+            vcp(("bw",), ("c2", 0, 14))
+            vcp(("sel",), ("sa", 0, 28, 2))
+        vts(("Tn",), ("t3",), 4095, A.bitwise_and)
+        if n < ST:
             op("v", [rg(z), ("AO", 14, 28)], [("XT", 0, NP)],
                lambda q: q.tensor_copy(T.XT[:, 0:NP].indirect(T.AO[:, 14:28]), ap(z)))
-
-    def clock():
-        vcp(("t1",), ("pW", 0, 14))
-        vts(("t2",), ("t1",), 31, A.bitwise_and)
-        vtt(("t3",), ("t2",), ("B1",), A.add)
-        vts(("Tn",), ("t3",), 4095, A.bitwise_and)
 
     def fetch(n):
         gat(("WA",), ("WT", 0, NP), ("AO", 0, 14))
         gat(("LG",), ("LT", 0, NP), ("AO", 0, 14))
-        mm(("pXR", 0, 224), ("ID",), ("BR",), n == 0, False)
+        br = ("BR", 0, 224) if n else row(0)
+        mm(("pXR", 0, 224), ("ID",), br, n == 0, False)
         for k, b in ((0, "pE"), (2, "pO")):
             o = (b, 0, 112)
             for h in range(2):
-                mm(o, mat("P4", k + h), ("BR", h, 224, 2), h == 0, False)
+                mm(o, mat("P4", k + h), (br[0], br[1] + h, br[2], 2), h == 0, False)
             if n:
                 for h in range(2):
                     mm(o, mat("BOE", h), ("ZS", 448 * n + h, 448 * n + 224, 2), False, False)
         mm(("pXR", 0, 224), ("ID",), ("WA",), False, True)
         vts(("KQ",), ("pXR", 0, 224), 1.0 / 32, A.mult, 1535.515625, A.add)
-        if n:
-            clock()
         vts(lst(n, "EF", 224, 238), ("Tn",), -2048.0, A.add)
-        for k, b, srcs in ((0, "pE", ("WA", "LG", "KQ")), (2, "pO", ("WA", "LG", "KQ"))):
-            for src in srcs:
-                for h in range(2):
-                    mm((b, 0, 112), mat({"WA": "P4", "LG": "P32", "KQ": "PM32"}[src], k + h), (src, h, 224, 2),
-                       False, src == "KQ" and h == 1)
-        vts(lst(n, "EO", 0, 112), ("pE", 0, 112), 45024.0, A.add)
-        vts(lst(n, "EO", 112, 224), ("pO", 0, 112), 45024.0, A.add)
-        vts(lst(n, "EF", 0, 224), lst(n, "EO", 0, 224), -1792.0, A.add)
+        for src, k in (("WA", 0), ("LG", 0), ("WA", 2), ("KQ", 0), ("LG", 2), ("KQ", 2)):
+            for h in range(2):
+                mm(("pO" if k else "pE", 0, 112), mat({"WA": "P4", "LG": "P32", "KQ": "PM32"}[src], k + h), (src, h, 224, 2),
+                   False, src == "KQ" and h == 1)
+        for b, lo, hi in (("pE", 0, 112), ("pO", 112, 224)):
+            vts(lst(n, "EO", lo, hi), (b, 0, 112), 45024.0, A.add)
+            vts(lst(n, "EF", lo, hi), (b, 0, 112), 43232.0, A.add)
 
     def big(n):
         for (a, b) in CH:
             gat(("VE", 16 * a, 16 * b), ("XT", 0, NP), lst(n, "EO", a, b))
-        mm(("pZ", 0, 224), ("NID",), zin(n), True, False)
+            if n and b == CH[RB][1]:
+                broadcast("pS", ("bw",), 256)
+                act(row(n), ("pS", 256, 480), AF.Copy)
+        y, last = zin(n), 2 * CH[-1][0]
+        mm(("pZ", 0, last), ("NID",), (y[0], y[1], y[1] + last), True, False)
+        mm(("pC", 256 + last, 480), ("NID",), (y[0], y[1] + last, y[2]), True, False)
 
         def least(a, b):
             off = lst(n, "EO", 112 + a, 112 + b)
@@ -353,11 +370,17 @@ def rank_program(g, core, T, topo):
             r = slice(16 * a, 16 * b)
             op("v", [("MASK", 16 * a, 16 * b), ("U", 16 * a, 16 * b)], [("M", 16 * a, 16 * b)],
                lambda q: q.tensor_tensor_scan(T.M[:, r], T.MASK[:, r], T.U[:, r], 0.0, A.min, A.max))
-            mm(("pZ", 2 * a, 2 * b), ("ID",), ("M", 16 * a + 7, 16 * b, 8), False, b == 112)
-        for c in CH:
+            o = ("pZ", 2 * a, 2 * b) if b < 112 else ("pC", 256 + 2 * a, 480)
+            mm(o, ("ID",), ("M", 16 * a + 7, 16 * b, 8), False, b == 112 or b == CH[-1][0])
+        for i, c in enumerate(CH):
             least(*c)
-            greatest(*c)
-        act(("ZO", 224 * n, 224 * n + 224), ("pZ", 0, 224), AF.Abs)
+            if i:
+                greatest(*CH[i - 1])
+        if n:
+            op("v", [("pW", 32, 46)], [("Ar", 0, 1)], lambda q: q.tensor_reduce(T.Ar[:], T.pW[:, 32:46], AxisListType.X, A.add))
+        greatest(*CH[-1])
+        act(("ZO", 224 * n, 224 * n + last), ("pZ", 0, last), AF.Abs)
+        act(("ZO", 224 * n + last, 224 * n + 224), ("pC", 256 + last, 480), AF.Abs)
 
     def ready(n):
         el = 240 * n
@@ -367,17 +390,11 @@ def rank_program(g, core, T, topo):
             mm(("pD", 224, 238), mat("SKD", t), ("EL", el + 112 + t, el + 224, 8), t == 0, t == 7)
         if n == 0:
             pick("SKA", 0)
-        for t in range(8):
-            mm(("pS", 0, 28), mat("SKA", t), ("EL", el + t, el + 224, 8), t == 0, t == 7)
-        if n:
-            op("v", [("pW", 32, 46)], [("Ar", 0, 1)], lambda q: q.tensor_reduce(T.Ar[:], T.pW[:, 32:46], AxisListType.X, A.add))
-            vcp(("Ai",), ("Ar",))
-            vts(("Aj",), ("Ai",), 31, A.bitwise_and)
-            vcp(("Af",), ("Aj",))
-            vts(("B1",), lst(n, "EL", 224, 238), ("Af", 0, 1), A.add, 2049.0, A.add)
-        else:
-            vts(("B1",), lst(n, "EL", 224, 238), 2049.0, A.add)
+            fill(("Ar",), 0.0)
+        vts(("KA",), ("Ar",), 1.0 / 32, A.mult, 191.515625, A.add)
+        vts(("Au",), ("KA",), -32.0, A.mult, 6145.0, A.add)
         vts(("DW",), ("pD", 224, 238), 1792.0, A.add)
+        vts(("A1",), ("Au",), ("Ar", 0, 1), A.add)
         vts(("DR",), ("pD", 0, 224), 1792.0, A.add)
         vcp(("DWu", 0, 14), ("DW",))
         gat(("DO",), ("WT", 0, NP), ("DWu", 0, 14))
@@ -387,50 +404,44 @@ def rank_program(g, core, T, topo):
             vts(e, ("DR", 16 * c, 224), ("DW", c, c + 1), A.is_equal)
             if c < 13:
                 mm(("pC", 16 * c + 16, 224), ("BIG",), (e[0], e[1] + 16, e[2]), False, False)
-            if c == 7:
-                vts(("bwi",), ("B1",), 31, A.bitwise_and)
-                vcp(("bw",), ("bwi",))
+            if c == 2:
+                vts(("B1",), lst(n, "EL", 224, 238), ("A1", 0, 1), A.add, 2048.0, A.add)
+            if c == 9:
+                vts(("KD",), ("DO",), 1.0 / 32, A.mult, 191.515625, A.add)
         mm(("pC", 0, 224), ("WQ",), ("EQ", 0, 14 * 240, 1), False, True)
-        vts(("KD",), ("DO",), 1.0 / 32, A.mult, 191.515625, A.add)
         mm(("pZ", 0, 224), ("ID",), ("DO",), True, False)
         mm(("pZ", 0, 224), ("NID32",), ("KD",), False, True)
         act(("DRED",), ("pZ", 0, 224), AF.Copy, bias=5984.0)
         mm(("pD", 256, 480), ("ID",), ye(n), True, True)
+        for t in range(8):
+            mm(("pS", 0, 28), mat("SKA", t), ("EL", el + t, el + 224, 8), t == 0, t == 7)
         vtt(("LF",), ("pC", 0, 224), ("thr",), A.is_gt)
-        op("v", [("RST", 0, 224), ("LF", 0, 224)], [("SC", 0, 224)],
-           lambda q: q.tensor_tensor_scan(T.SC[:], T.RST[:], T.LF[:], 0.0, A.mult, A.add))
-        vtt(("o1",), ("SC", 15, 224, 16), ("trash",), A.mult)
-        vtt(("o2",), ("o1",), ("DW",), A.max)
-        vcp(("OFF", 0, 14), ("o2",))
-        vts(("SI",), ("pS", 0, 28), 1792.0, A.add)
-        vts(("SJ",), ("SI",), 4064, A.bitwise_and)
-        vtt(("dL",), ("SJ", 14, 28), ("SJ", 0, 14), A.subtract)
+        op("v", [("trm", 0, 224), ("LF", 0, 224)], [("SC", 0, 224)],
+           lambda q: q.tensor_tensor_scan(T.SC[:], T.trm[:], T.LF[:], 0.0, A.max, A.mult))
         if n < ST - 1:
-            broadcast("pS", ("bw",), 256)
-            act(("BR",), ("pS", 256, 480), AF.Copy)
+            op("s", [(ye(n)[0], ye(n)[2], ye(n)[2] + 224), ("A1", 0, 1)], [("BR", 0, 224)],
+               lambda q: q.activation(T.BR[:], T.YE[:, 448 * n + 224:448 * n + 448], AF.Identity, bias=T.A1[:]))
 
     for n in range(ST):
         if n:
             arrive(n)
-        send(ye(n), zin(n), "ay%d" % n)
         fetch(n)
         if n:
             mm(("pW", 32, 46), ("ONE",), ("sel",), True, True)
         send(lst(n, "EL", 0, 238), lst(n, "EF", 0, 238), "ae%d" % n)
         big(n)
+        send(("YE", 448 * n, 448 * n + 448), ("ZS", 448 * n, 448 * n + 448), "ay%d" % n)
         send(zin(n + 1), ("ZO", 224 * n, 224 * n + 224), "az%d" % n)
         ready(n)
 
     dma("y", [rg(zin(ST))], [], T.yy[:], ap(zin(ST)), "d_o0")
-    rewrite(zin(ST))
     arrive(ST)
     for i in range(7):
         lo, hi = 512 * i, 512 * i + 512
         vts(("KF", lo, hi), ("WT", lo, hi), 1.0 / 32, A.mult, 191.515625, A.add)
         if i == 1:
-            clock()
             vts(("fo", 0, 14), ("Tn",), -2048.0, A.add)
-            vtt(("fo", 14, 28), ("ldel",), ("SJ", 0, 14), A.add)
+            vcp(("fo", 14, 28), ("lin", 1, 28, 2))
             for r in range(16):
                 mm(("pS", r, 448, 16), mat("BC", r), ("fo",), True, True)
         if i in (3, 6):

@@ -2,7 +2,8 @@ from concourse.mybir import AluOpType as A, AxisListType, ActivationFunctionType
 
 NP, NB, NR, ST = 3584, 224, 4, 8
 RB = 3
-CH = [(0, 14), (14, 30), (30, 50), (50, 74), (74, 98), (98, 112)]
+CUT = 96
+CH = [(0, 12), (12, 28), (28, 48), (48, 74), (74, 98), (98, 112)]
 
 
 def _sb(dtype, **widths):
@@ -111,6 +112,8 @@ def rank_program(g, core, T, topo):
         return T[o[0]][:, o[1]:o[2]]
 
     def rg(o):
+        if o[0] == "sa":
+            return ("sa%d" % (o[1] % 2), 0, 28)
         return (o[0], 0, SCRATCH[o[0]][1][1]) if len(o) == 1 else (o[0], o[1], o[2])
 
     def vts(out, i, s1, o0, s2=None, o1=None):
@@ -196,27 +199,30 @@ def rank_program(g, core, T, topo):
     def asel(out, i, pat, cmp, base, cm, other=0.0):
         op("p", [rg(i)], [rg(out)], lambda q: q.affine_select(ap(out), ap(i), pat, cmp, other, base, cm))
     asel(("BO0",), ("ONE",), [[-16, 8], [0, 16]], A.is_ge, 0, 1)
-    asel(("BO",), ("BO0",), [[16, 8], [0, 16]], A.is_ge, 15, -1)
     asel(("ID",), ("ONE",), [[-1, 128]], A.is_equal, 0, 1)
+    asel(("BO",), ("BO0",), [[16, 8], [0, 16]], A.is_ge, 15, -1)
+    fill(("SEL",), 0.0)
+    asel(("SKD",), ("SEL", 0, 1024), [[0, 1024]], A.is_ge, -1, 0)
     asel(mat("BOE", 0), ("BO",), [[0, 8], [-1, 16]], A.is_ge, 7, 0)
     asel(mat("BOE", 1), ("BO",), [[0, 8], [1, 16]], A.is_ge, -8, 0)
     for k, (h, base) in enumerate(((0, 0), (1, 16), (0, -1), (1, 15))):
         asel(mat("P4", k), mat("BOE", h), [[-16, 8], [-2, 16]], A.is_equal, base, 1)
     op("p", [], [("iw", 0, 14)], lambda q: q.iota(T.iw[:], [[16, 14]], 0, 1))
     op("p", [], [("ip", 0, 14)], lambda q: q.iota(T.ip[:], [[0, 14]], 0, 1))
-    fill(("SEL",), 0.0)
     for r in range(16):
-        vcp(("SEL", 128 * r + r, 128 * r + 128, 16), ("BO", r, 128, 16))
+        fill(("th16", r, r + 1), 2.0 * 4.0 ** (15 - r))
     vts(("NID32",), ("ID",), -32.0, A.mult)
-    for m in ("SKD", "SKA"):
-        asel((m,), ("SEL", 0, 1024), [[0, 1024]], A.is_ge, -1, 0)
+    asel(("SKA",), ("SKD",), [[0, 1024]], A.is_ge, -1, 0)
     asel(("ZER",), ("ID",), [[0, 128]], A.is_ge, -1, 0)
     for k in range(2):
         asel(("MASK", 896 * k, 896 * k + 896), ("SKA", 0, 896), [[0, 112], [1, 8]], A.is_equal, 0, 0, 256.0)
 
-    def table(i):
+    def halves(i):
         lo, hi = 512 * i, 512 * i + 512
         vts(("f16t", lo, hi), ("ilb", lo, hi), -1792.0, A.add)
+
+    def table(i):
+        lo, hi = 512 * i, 512 * i + 512
         vts(("LT", lo, hi), ("f16t", lo, hi), 1.0 / 32, A.mult, 184.515625, A.add)
         pb = ("pXR", "pE", "pO", "pZ")[i % 4]
         mm((pb,), ("ID",), ("f16t", lo, hi), True, False)
@@ -245,57 +251,86 @@ def rank_program(g, core, T, topo):
             mm((dst, r + lo, lo + 224, 16), mat("BC", r), src, True, True)
 
     def pick(m, k):
-        for t in range(8):
-            for h in range(2):
+        for h in range(2):
+            for t in range(8):
                 act((m, 128 * t + 2 * t + h, 128 * t + 128, 16), ("ID", k + 8 * h, 128, 16), AF.Copy)
 
     def weights():
-        for r in range(16):
-            fill(("th16", r, r + 1), 2.0 * 4.0 ** (15 - r))
+        op("p", [], [("trm", 0, 224)], lambda q: q.iota(T.trm[:], [[1, 224]], NP, 0, allow_small_or_imprecise_dtypes=True))
         vtt(("rq",), ("rm",), ("th16",), A.mult)
-        op("v", [("rq", 0, 16)], [("wq1", 0, 1)], lambda q: q.tensor_reduce(T.wq1[:], T.rq[:], AxisListType.X, A.add))
-        vts(("WQ",), ("BO",), ("wq1", 0, 1), A.mult, 0.5, A.mult)
-        vts(("BIG",), ("BO",), 2.0 ** 32, A.mult)
         vcp(("DG", 0, 16), ("rm",))
-        for a, b in ((16, 16), (32, 32), (64, 64), (128, 96)):
-            vcp(("DG", a, a + b), ("DG", 0, b))
+        vts(("ipq",), ("ip",), 112, A.bitwise_and)
+        vts(("BIG",), ("BO",), 2.0 ** 32, A.mult)
+        op("v", [("rq", 0, 16)], [("wq1", 0, 1)], lambda q: q.tensor_reduce(T.wq1[:], T.rq[:], AxisListType.X, A.add))
+        vcp(("DG", 16, 32), ("DG", 0, 16))
+        vtt(("iw",), ("iw",), ("ipq",), A.subtract)
+        fill(("sd",), 0.0)
+        fill(("Ar",), 0.0)
+        vcp(("DG", 32, 64), ("DG", 0, 32))
+        vts(("WQ",), ("BO",), ("wq1", 0, 1), A.mult, 0.5, A.mult)
+        vts(("b2", 14, 28), ("iw",), 16.0, A.mult)
+        vcp(("DG", 64, 128), ("DG", 0, 64))
+        vts(("NID",), ("ID",), -1.0, A.mult)
+        vcp(("DG", 128, 224), ("DG", 0, 96))
         vts(("thA",), ("DG",), ("wq1", 0, 1), A.mult)
         vts(("thB",), ("DG",), 1.0, A.subtract)
-        vtt(("thr",), ("thA",), ("thB",), A.add)
-        vts(("ipq",), ("ip",), 112, A.bitwise_and)
-        vtt(("iw",), ("iw",), ("ipq",), A.subtract)
-        vts(("b2", 14, 28), ("iw",), 16.0, A.mult)
-        op("p", [], [("trm", 0, 224)], lambda q: q.iota(T.trm[:], [[1, 224]], NP, 0, allow_small_or_imprecise_dtypes=True))
         vtt(("trm",), ("trm",), ("DG",), A.mult)
-        fill(("sd",), 0.0)
+        vtt(("thr",), ("thA",), ("thB",), A.add)
 
-    table(0)
+    halves(0)
     vtt(("h64",), ("ID", 0, 64), ("ID", 64, 128), A.add)
+    halves(1)
     vtt(("h32",), ("h64", 0, 32), ("h64", 32, 64), A.add)
+    table(0)
     vtt(("rm",), ("h32", 0, 16), ("h32", 16, 32), A.add)
-    table(1)
+    halves(2)
     for r in range(16):
         act(mat("BC", r), ("BO",), AF.Copy, scale=T.rm[:, r:r + 1])
+    table(1)
+    for r in range(16):
+        vcp(("SEL", 128 * r + r, 128 * r + 128, 16), ("BO", r, 128, 16))
+    halves(3)
     table(2)
+    halves(4)
     table(3)
-    clocks()
+    halves(5)
     table(4)
-    pick("SKD", 7)
-    places()
+    clocks()
+    halves(6)
     table(5)
+    pick("SKD", 7)
     table(6)
+    places()
     broadcast("pS", ("bw",), 256)
     act(row(0), ("pS", 256, 480), AF.Copy)
     vts(("PM32",), ("P4",), -32.0, A.mult)
     vts(("P32",), ("P4",), 32.0, A.mult)
-    vts(("NID",), ("ID",), -1.0, A.mult)
     weights()
+
+    def reduced(i, k):
+        lo, hi = 512 * i, 512 * i + 512
+        if k == 0:
+            vts(("KF", lo, hi), ("WT", lo, hi), 1.0 / 32, A.mult, 191.515625, A.add)
+        elif k == 1:
+            pb = ("pE", "pO", "pZ")[i % 3]
+            mm((pb,), ("ID",), ("WT", lo, hi), True, False)
+            mm((pb,), ("NID32",), ("KF", lo, hi), False, True)
+            act(("YW", lo, hi), (pb,), AF.Copy, bias=6144.0)
+        elif k == 2:
+            vts(("f16t", lo, hi), ("KF", lo, hi), -32.0, A.mult, 6144.0, A.add)
+        else:
+            vtt(("YW", lo, hi), ("WT", lo, hi), ("f16t", lo, hi), A.add)
+        if k % 2:
+            dma("y", [("YW", lo, hi)], [], T.yw[:, lo:hi], T.YW[:, lo:hi], "d_o%d" % (1 + i))
+
+    def more(n, i):
+        if n == ST:
+            reduced(i, 0)
+            reduced(i, 1)
 
     def arrive(n):
         z = zin(n)
         vtt(("ZS", 448 * n + 224, 448 * n + 448), z, ("pD", 256, 480), A.is_ge)
-        if n < ST:
-            mm(("pXR", 0, 224), ("BO",), z, True, False)
         for r in range(16):
             mm(("pW", 0, 28), mat("SEL", r), ("ZS", 448 * n + r, 448 * n + 448, 16), r == 0, r == 15)
         vtt(("o2",), ("SC", 15, 224, 16), ("DW",), A.max)
@@ -304,52 +339,80 @@ def rank_program(g, core, T, topo):
         vts(("SJ",), ("SI",), 4064, A.bitwise_and)
         op("v", [rg(z), ("DRED", 0, 224), ("OFF", 0, 14)], [("WT", 0, NP + NB)],
            lambda q: q.tensor_tensor(T.WT[:, 0:NP + NB].indirect(T.OFF[:, 0:14]), T.DRED[:], ap(z), A.add))
+        more(n, 0)
+        more(n, 1)
         vtt(("sd", 1, 28, 2), ("SJ", 14, 28), ("SJ", 0, 14), A.subtract)
         vcp(("sa", 1, 28, 2), ("SJ", 0, 14))
-        vtt(("q",), ("pW", 0, 14), ("B1",), A.add)
         vts(("sa", 0, 28, 2), ("pW", 14, 28), 9.0, A.is_ge)
+        if n < ST:
+            vtt(("q",), ("pW", 0, 14), ("B1",), A.add)
         vcp(("t1",), ("pW", 0, 14))
+        more(n, 2)
+        op("v", [("sd", 0, 28), ("sa0", 0, 28), ("sa1", 0, 28)], [("lin", 0, 28)],
+           lambda q: q.tensor_tensor_scan(T.lin[:], T.sd[:], T.sa[:], 0.0, A.mult, A.add))
         if n < ST:
             vts(("c2", 0, 14), ("q",), 31, A.bitwise_and)
             vts(("c2", 14, 28), ("q",), 15, A.bitwise_and)
-        op("v", [("sd", 0, 28), ("sa", 0, 28)], [("lin", 0, 28)],
-           lambda q: q.tensor_tensor_scan(T.lin[:], T.sd[:], T.sa[:], 0.0, A.mult, A.add))
         vts(("t2",), ("t1",), 31, A.bitwise_and)
         if n < ST:
             vtt(("ao", 14, 28), ("c2", 14, 28), ("b2", 14, 28), A.add)
             vtt(("ao", 0, 14), ("c2", 0, 14), ("lin", 1, 28, 2), A.add)
+        more(n, 3)
         vtt(("t3",), ("t2",), ("B1",), A.add)
         if n < ST:
             vcp(("AO",), ("ao",))
             vcp(("bw",), ("c2", 0, 14))
             vcp(("sel",), ("sa", 0, 28, 2))
+        more(n, 4)
         vts(("Tn",), ("t3",), 4095, A.bitwise_and)
         if n < ST:
             op("v", [rg(z), ("AO", 14, 28)], [("XT", 0, NP)],
                lambda q: q.tensor_copy(T.XT[:, 0:NP].indirect(T.AO[:, 14:28]), ap(z)))
 
     def fetch(n):
-        gat(("WA",), ("WT", 0, NP), ("AO", 0, 14))
-        gat(("LG",), ("LT", 0, NP), ("AO", 0, 14))
-        br = ("BR", 0, 224) if n else row(0)
-        mm(("pXR", 0, 224), ("ID",), br, n == 0, False)
-        for k, b in ((0, "pE"), (2, "pO")):
-            o = (b, 0, 112)
+        parts = ((0, CUT, "pXR", ("pE", "pO")), (CUT, NB, "pC", ("pD", "pS")))
+        br = ("BR", 0) if n else row(0)[:2]
+
+        def x(o, lo, hi, h=None):
+            return (o[0], o[1] + lo, o[1] + hi) if h is None else (o[0], o[1] + lo + h, o[1] + hi, 2)
+
+        def lists(part, src, k):
+            lo, hi, _, banks = parts[part]
             for h in range(2):
-                mm(o, mat("P4", k + h), (br[0], br[1] + h, br[2], 2), h == 0, False)
+                mm((banks[k // 2], lo // 2, hi // 2), mat({"WA": "P4", "LG": "P32", "KQ": "PM32"}[src], k + h),
+                   x((src, 0), lo, hi, h), False, src == "KQ" and h == 1)
+
+        def floors(part):
+            lo, hi, b, _ = parts[part]
+            mm((b, lo, hi), ("ID",), ("WA", lo, hi), False, True)
+            vts(("KQ", lo, hi), (b, lo, hi), 1.0 / 32, A.mult, 1535.515625, A.add)
+
+        for lo, hi, b, banks in parts:
+            gat(("WA", lo, hi), ("WT", 0, NP), ("AO", lo // 16, hi // 16))
+            gat(("LG", lo, hi), ("LT", 0, NP), ("AO", lo // 16, hi // 16))
+            mm((b, lo, hi), ("ID",), x(br, lo, hi), True, False)
             if n:
+                mm((b, lo, hi), ("BO",), x(zin(n), lo, hi), False, False)
+        for lo, hi, b, banks in parts:
+            for k in (0, 2):
                 for h in range(2):
-                    mm(o, mat("BOE", h), ("ZS", 448 * n + h, 448 * n + 224, 2), False, False)
-        mm(("pXR", 0, 224), ("ID",), ("WA",), False, True)
-        vts(("KQ",), ("pXR", 0, 224), 1.0 / 32, A.mult, 1535.515625, A.add)
+                    mm((banks[k // 2], lo // 2, hi // 2), mat("P4", k + h), x(br, lo, hi, h), h == 0, False)
+                for h in range(2 if n else 0):
+                    mm((banks[k // 2], lo // 2, hi // 2), mat("BOE", h), x(zin(n), lo, hi, h), False, False)
+        floors(0)
         vts(lst(n, "EF", 224, 238), ("Tn",), -2048.0, A.add)
-        for src, k in (("WA", 0), ("LG", 0), ("WA", 2), ("KQ", 0), ("LG", 2), ("KQ", 2)):
-            for h in range(2):
-                mm(("pO" if k else "pE", 0, 112), mat({"WA": "P4", "LG": "P32", "KQ": "PM32"}[src], k + h), (src, h, 224, 2),
-                   False, src == "KQ" and h == 1)
-        for b, lo, hi in (("pE", 0, 112), ("pO", 112, 224)):
-            vts(lst(n, "EO", lo, hi), (b, 0, 112), 45024.0, A.add)
-            vts(lst(n, "EF", lo, hi), (b, 0, 112), 43232.0, A.add)
+        lists(0, "WA", 0)
+        lists(0, "LG", 0)
+        lists(0, "WA", 2)
+        floors(1)
+        for src, k in (("KQ", 0), ("LG", 2), ("KQ", 2)):
+            lists(0, src, k)
+        for src, k in (("WA", 0), ("LG", 0), ("KQ", 0), ("WA", 2), ("LG", 2), ("KQ", 2)):
+            lists(1, src, k)
+        for lo, hi, _, banks in parts:
+            for b, o in ((banks[0], 0), (banks[1], 112)):
+                vts(lst(n, "EO", o + lo // 2, o + hi // 2), (b, lo // 2, hi // 2), 45024.0, A.add)
+                vts(lst(n, "EF", o + lo // 2, o + hi // 2), (b, lo // 2, hi // 2), 43232.0, A.add)
 
     def big(n):
         for (a, b) in CH:
@@ -390,7 +453,6 @@ def rank_program(g, core, T, topo):
             mm(("pD", 224, 238), mat("SKD", t), ("EL", el + 112 + t, el + 224, 8), t == 0, t == 7)
         if n == 0:
             pick("SKA", 0)
-            fill(("Ar",), 0.0)
         vts(("KA",), ("Ar",), 1.0 / 32, A.mult, 191.515625, A.add)
         vts(("Au",), ("KA",), -32.0, A.mult, 6145.0, A.add)
         vts(("DW",), ("pD", 224, 238), 1792.0, A.add)
@@ -436,30 +498,16 @@ def rank_program(g, core, T, topo):
 
     dma("y", [rg(zin(ST))], [], T.yy[:], ap(zin(ST)), "d_o0")
     arrive(ST)
-    for i in range(7):
-        lo, hi = 512 * i, 512 * i + 512
-        vts(("KF", lo, hi), ("WT", lo, hi), 1.0 / 32, A.mult, 191.515625, A.add)
-        if i == 1:
-            vts(("fo", 0, 14), ("Tn",), -2048.0, A.add)
-            vcp(("fo", 14, 28), ("lin", 1, 28, 2))
-            for r in range(16):
-                mm(("pS", r, 448, 16), mat("BC", r), ("fo",), True, True)
-        if i in (3, 6):
-            vts(("f16t", lo, hi), ("KF", lo, hi), -32.0, A.mult, 6144.0, A.add)
-            vtt(("YW", lo, hi), ("WT", lo, hi), ("f16t", lo, hi), A.add)
-        else:
-            pb = ("pE", "pO", "pZ")[i % 3]
-            mm((pb,), ("ID",), ("WT", lo, hi), True, False)
-            mm((pb,), ("NID32",), ("KF", lo, hi), False, True)
-            act(("YW", lo, hi), (pb,), AF.Copy, bias=6144.0)
-        if i == 3:
-            vts(("fr", 0, 224), ("pS", 0, 224), 2048.0, A.add)
-            vts(("fr", 224, 448), ("pS", 224, 448), 1.0 / 32, A.mult)
-            dma("y", [("fr", 0, 224)], [], T.yt[:], T.fr[0:128:16, 0:224], "d_t")
-            dma("y", [("fr", 224, 448)], [], T.yl[:], T.fr[0:128:16, 224:448], "d_l")
-    for i in range(7):
-        lo, hi = 512 * i, 512 * i + 512
-        dma("y", [("YW", lo, hi)], [], T.yw[:, lo:hi], T.YW[:, lo:hi], "d_o%d" % (1 + i))
+    vts(("fo", 0, 14), ("Tn",), -2048.0, A.add)
+    vcp(("fo", 14, 28), ("lin", 1, 28, 2))
+    for r in range(16):
+        mm(("pS", r, 448, 16), mat("BC", r), ("fo",), True, True)
+    for i, k in ((5, 0), (6, 0), (5, 2), (6, 2), (5, 3), (6, 3)):
+        reduced(i, k)
+    vts(("fr", 0, 224), ("pS", 0, 224), 2048.0, A.add)
+    vts(("fr", 224, 448), ("pS", 224, 448), 1.0 / 32, A.mult)
+    dma("s", [("fr", 0, 224)], [], T.yt[:], T.fr[0:128:16, 0:224], "d_t")
+    dma("s", [("fr", 224, 448)], [], T.yl[:], T.fr[0:128:16, 224:448], "d_l")
     for s in SEMAPHORES:
         if count[s] and known["p"].get(s, 0) < count[s]:
             g.wait_ge(T.sem[s], count[s])

@@ -2,8 +2,9 @@ from concourse.mybir import AluOpType as A, AxisListType, ActivationFunctionType
 
 NP, NB, NR, ST = 3584, 224, 4, 8
 RB = 3
+LATE = 4
 CUT = 96
-CH = [(0, 12), (12, 28), (28, 48), (48, 74), (74, 98), (98, 112)]
+CH = [(0, 12), (12, 28), (28, 48), (48, 72), (72, 92), (92, 112)]
 
 
 def _sb(dtype, **widths):
@@ -26,7 +27,7 @@ SCRATCH = {
 }
 SEMAPHORES = (["cv", "ct", "cs", "cp", "loc", "d_tk", "d_ln", "d_y", "d_x0", "d_x1", "d_t", "d_l"]
               + ["d_il%d" % i for i in range(7)] + ["d_o%d" % i for i in range(8)]
-              + ["a%s%d" % (k, n) for k in "zye" for n in range(ST)])
+              + ["a%s%d" % (k, n) for k in "zbye" for n in range(ST)])
 
 
 def rank_program(g, core, T, topo):
@@ -104,7 +105,7 @@ def rank_program(g, core, T, topo):
     def ap(o):
         if o[0] == "EQ":
             c, a = divmod(o[1], 240)
-            return T.EQ[:, c, a:a + o[2] - o[1]] if len(o) == 3 else T.EQ[:, :, 0:16]
+            return T.EQ[:, c, a:a + o[2] - o[1]] if len(o) == 3 else T.EQ[:, c:o[2] // 240, 0:16]
         if len(o) == 1:
             return T[o[0]][:]
         if len(o) == 4:
@@ -173,6 +174,9 @@ def rank_program(g, core, T, topo):
     def ye(n):
         return ("YE", 448 * n, 448 * n + 224)
 
+    def zparts(b, lo, hi):
+        return (b, lo, lo + 2 * CH[LATE][0]), (b, lo + 2 * CH[LATE][0], hi)
+
     def row(n):
         return ("ZS", 448 * n + 224, 448 * n + 448)
 
@@ -182,7 +186,8 @@ def rank_program(g, core, T, topo):
     for n in range(ST):
         lands(("YE", 448 * n, 448 * n + 448), "ay%d" % n)
         lands(lst(n, "EL", 0, 238), "ae%d" % n)
-        lands(zin(n + 1), "az%d" % n)
+        for z, s in zip(zparts(*zin(n + 1)), "zb"):
+            lands(z, "a%s%d" % (s, n))
 
     fill(("TLi",), 0)
     fill(("ONE",), 1.0)
@@ -274,9 +279,9 @@ def rank_program(g, core, T, topo):
         vcp(("DG", 128, 224), ("DG", 0, 96))
         vts(("thA",), ("DG",), ("wq1", 0, 1), A.mult)
         vts(("thB",), ("DG",), 1.0, A.subtract)
-        vtt(("trm",), ("trm",), ("DG",), A.mult)
-        vtt(("thr",), ("thA",), ("thB",), A.add)
 
+    for r in range(16):
+        act(("SEL", 128 * r + r, 128 * r + 128, 16), ("BO", r, 128, 16), AF.Copy)
     halves(0)
     vtt(("h64",), ("ID", 0, 64), ("ID", 64, 128), A.add)
     halves(1)
@@ -287,8 +292,6 @@ def rank_program(g, core, T, topo):
     for r in range(16):
         act(mat("BC", r), ("BO",), AF.Copy, scale=T.rm[:, r:r + 1])
     table(1)
-    for r in range(16):
-        vcp(("SEL", 128 * r + r, 128 * r + 128, 16), ("BO", r, 128, 16))
     halves(3)
     table(2)
     halves(4)
@@ -355,12 +358,13 @@ def rank_program(g, core, T, topo):
             vts(("c2", 14, 28), ("q",), 15, A.bitwise_and)
         vts(("t2",), ("t1",), 31, A.bitwise_and)
         if n < ST:
-            vtt(("ao", 14, 28), ("c2", 14, 28), ("b2", 14, 28), A.add)
             vtt(("ao", 0, 14), ("c2", 0, 14), ("lin", 1, 28, 2), A.add)
+            vtt(("ao", 14, 28), ("c2", 14, 28), ("b2", 14, 28), A.add)
         more(n, 3)
         vtt(("t3",), ("t2",), ("B1",), A.add)
         if n < ST:
-            vcp(("AO",), ("ao",))
+            vcp(("AO", 0, 14), ("ao", 0, 14))
+            vcp(("AO", 14, 28), ("ao", 14, 28))
             vcp(("bw",), ("c2", 0, 14))
             vcp(("sel",), ("sa", 0, 28, 2))
         more(n, 4)
@@ -420,9 +424,10 @@ def rank_program(g, core, T, topo):
             if n and b == CH[RB][1]:
                 broadcast("pS", ("bw",), 256)
                 act(row(n), ("pS", 256, 480), AF.Copy)
-        y, last = zin(n), 2 * CH[-1][0]
-        mm(("pZ", 0, last), ("NID",), (y[0], y[1], y[1] + last), True, False)
-        mm(("pC", 256 + last, 480), ("NID",), (y[0], y[1] + last, y[2]), True, False)
+        last = 2 * CH[LATE][0]
+        early, late = zparts(*zin(n))
+        mm(("pZ", 0, last), ("NID",), early, True, False)
+        mm(("pC", 256 + last, 480), ("NID",), late, True, False)
 
         def least(a, b):
             off = lst(n, "EO", 112 + a, 112 + b)
@@ -433,8 +438,8 @@ def rank_program(g, core, T, topo):
             r = slice(16 * a, 16 * b)
             op("v", [("MASK", 16 * a, 16 * b), ("U", 16 * a, 16 * b)], [("M", 16 * a, 16 * b)],
                lambda q: q.tensor_tensor_scan(T.M[:, r], T.MASK[:, r], T.U[:, r], 0.0, A.min, A.max))
-            o = ("pZ", 2 * a, 2 * b) if b < 112 else ("pC", 256 + 2 * a, 480)
-            mm(o, ("ID",), ("M", 16 * a + 7, 16 * b, 8), False, b == 112 or b == CH[-1][0])
+            o = ("pZ", 2 * a, 2 * b) if 2 * b <= last else ("pC", 256 + 2 * a, 256 + 2 * b)
+            mm(o, ("ID",), ("M", 16 * a + 7, 16 * b, 8), False, 2 * b in (last, 224))
         for i, c in enumerate(CH):
             least(*c)
             if i:
@@ -442,44 +447,64 @@ def rank_program(g, core, T, topo):
         if n:
             op("v", [("pW", 32, 46)], [("Ar", 0, 1)], lambda q: q.tensor_reduce(T.Ar[:], T.pW[:, 32:46], AxisListType.X, A.add))
         greatest(*CH[-1])
-        act(("ZO", 224 * n, 224 * n + last), ("pZ", 0, last), AF.Abs)
-        act(("ZO", 224 * n + last, 224 * n + 224), ("pC", 256 + last, 480), AF.Abs)
+        out = zparts("ZO", 224 * n, 224 * n + 224)
+        act(out[0], ("pZ", 0, last), AF.Abs)
+        act(out[1], ("pC", 256 + last, 480), AF.Abs)
+        send(("YE", 448 * n, 448 * n + 448), ("ZS", 448 * n, 448 * n + 448), "ay%d" % n)
+        for d, o, s in zip(zparts(*zin(n + 1)), out, "zb"):
+            send(d, o, "a%s%d" % (s, n))
 
     def ready(n):
         el = 240 * n
         for k in (7, 15):
             mm(("pD", k // 8, 224, 2), mat("BC", k), ("EL", el + 112, el + 224), True, True)
         for t in range(8):
-            mm(("pD", 224, 238), mat("SKD", t), ("EL", el + 112 + t, el + 224, 8), t == 0, t == 7)
+            mm(("pS", 32, 46), mat("SKD", t), ("EL", el + 112 + t, el + 224, 8), t == 0, t == 7)
         if n == 0:
             pick("SKA", 0)
+            vtt(("trm",), ("trm",), ("DG",), A.mult)
+            vtt(("thr",), ("thA",), ("thB",), A.add)
         vts(("KA",), ("Ar",), 1.0 / 32, A.mult, 191.515625, A.add)
         vts(("Au",), ("KA",), -32.0, A.mult, 6145.0, A.add)
-        vts(("DW",), ("pD", 224, 238), 1792.0, A.add)
-        vts(("A1",), ("Au",), ("Ar", 0, 1), A.add)
         vts(("DR",), ("pD", 0, 224), 1792.0, A.add)
+        vts(("DW",), ("pS", 32, 46), 1792.0, A.add)
+        vts(("A1",), ("Au",), ("Ar", 0, 1), A.add)
         vcp(("DWu", 0, 14), ("DW",))
         gat(("DO",), ("WT", 0, NP), ("DWu", 0, 14))
-        mm(("pC", 0, 224), ("ZER",), ("MASK", 0, 224), True, False)
+        half = (("pC", 0, 112), ("pE", 112, 224))
+        for b, lo, hi in half:
+            mm((b, lo, hi), ("ZER",), ("MASK", lo, hi), True, False)
+
+        def strips(h):
+            mm(half[h], ("WQ",), ("EQ", 7 * 240 * h, 7 * 240 * (h + 1), 1), False, True)
+
+        def losers(h):
+            b, lo, hi = half[h]
+            vtt(("LF", lo, hi), (b, lo, hi), ("thr", lo, hi), A.is_gt)
+            op("v", [("trm", lo, hi), ("LF", lo, hi)], [("SC", lo, hi)],
+               lambda q: q.tensor_tensor_scan(T.SC[:, lo:hi], T.trm[:, lo:hi], T.LF[:, lo:hi], 0.0, A.max, A.mult))
+
         for c in range(14):
             e = ("EQ", 240 * c, 240 * c + 224 - 16 * c)
             vts(e, ("DR", 16 * c, 224), ("DW", c, c + 1), A.is_equal)
-            if c < 13:
-                mm(("pC", 16 * c + 16, 224), ("BIG",), (e[0], e[1] + 16, e[2]), False, False)
+            for b, lo, hi in half:
+                lo = max(lo, 16 * c + 16)
+                if lo < hi:
+                    mm((b, lo, hi), ("BIG",), (e[0], e[1] + lo - 16 * c, e[1] + hi - 16 * c), False, False)
+            if c % 7 == 6:
+                strips(c // 7)
             if c == 2:
                 vts(("B1",), lst(n, "EL", 224, 238), ("A1", 0, 1), A.add, 2048.0, A.add)
             if c == 9:
                 vts(("KD",), ("DO",), 1.0 / 32, A.mult, 191.515625, A.add)
-        mm(("pC", 0, 224), ("WQ",), ("EQ", 0, 14 * 240, 1), False, True)
+        losers(0)
+        losers(1)
         mm(("pZ", 0, 224), ("ID",), ("DO",), True, False)
         mm(("pZ", 0, 224), ("NID32",), ("KD",), False, True)
         act(("DRED",), ("pZ", 0, 224), AF.Copy, bias=5984.0)
         mm(("pD", 256, 480), ("ID",), ye(n), True, True)
         for t in range(8):
             mm(("pS", 0, 28), mat("SKA", t), ("EL", el + t, el + 224, 8), t == 0, t == 7)
-        vtt(("LF",), ("pC", 0, 224), ("thr",), A.is_gt)
-        op("v", [("trm", 0, 224), ("LF", 0, 224)], [("SC", 0, 224)],
-           lambda q: q.tensor_tensor_scan(T.SC[:], T.trm[:], T.LF[:], 0.0, A.max, A.mult))
         if n < ST - 1:
             op("s", [(ye(n)[0], ye(n)[2], ye(n)[2] + 224), ("A1", 0, 1)], [("BR", 0, 224)],
                lambda q: q.activation(T.BR[:], T.YE[:, 448 * n + 224:448 * n + 448], AF.Identity, bias=T.A1[:]))
@@ -492,8 +517,6 @@ def rank_program(g, core, T, topo):
             mm(("pW", 32, 46), ("ONE",), ("sel",), True, True)
         send(lst(n, "EL", 0, 238), lst(n, "EF", 0, 238), "ae%d" % n)
         big(n)
-        send(("YE", 448 * n, 448 * n + 448), ("ZS", 448 * n, 448 * n + 448), "ay%d" % n)
-        send(zin(n + 1), ("ZO", 224 * n, 224 * n + 224), "az%d" % n)
         ready(n)
 
     dma("y", [rg(zin(ST))], [], T.yy[:], ap(zin(ST)), "d_o0")

from concourse.mybir import AluOpType as A, AxisListType, ActivationFunctionType as AF

NP, NB, NR, ST = 3584, 224, 4, 8
RB = 3
LATE = 4
CUT = 96
CH = [(0, 12), (12, 28), (28, 48), (48, 72), (72, 92), (92, 112)]


def _sb(dtype, **widths):
    return {n: ("sbuf", [128, w], dtype) for n, w in widths.items()}


SCRATCH = {
    **_sb("int32", ilb=NP, TLi=2 * NB, TLj=2 * NB, iw=14, ip=14, ipq=14, SI=28, SJ=28, q=14, c2=28, b2=28, ao=28,
          t1=14, t2=14, t3=14, Tn=14, B1=14),
    **_sb("float16", f16t=NP, PM32=512, EF=8 * 240, EL=8 * 240, KQ=NB, fo=28),
    **_sb("uint16", EO=8 * 240, DR=NB, DWu=16, OFF=16, AO=28),
    **_sb("float32", h64=64, h32=32, rm=16, rq=16, wq1=1, th16=16, DG=NB, thA=NB, thB=NB, thr=NB, trm=NB, SC=NB, DW=14,
          o2=14, sd=28, sa=28, lin=28, Ar=1, Au=1, A1=1, fr=2 * NB),
    **_sb("bfloat16", XT=NP, LT=NP, WT=NP + NB, YW=NP, KF=NP, TLb=3 * NB, ONE=128, ZER=128, BO0=128, BO=128, BOE=256,
          ID=128, NID=128, NID32=128, P4=512, P32=512, SEL=2048, BC=2048, SKA=1024, SKD=1024, WQ=128, BIG=128,
          MASK=1792, ZS=9 * 448, ZO=8 * NB, YE=8 * 448, LF=NB, KA=1, DO=NB, KD=NB, DRED=NB, sel=14, bw=14,
          BR=NB, WA=NB, LG=NB, VE=1792, U=1792, M=1792),
    "EQ": ("sbuf", [128, 14, 240], "bfloat16"),
    **{n: ("psum", [128, 512], "float32") for n in ("pXR", "pE", "pO", "pZ", "pW", "pS", "pD", "pC")},
}
SEMAPHORES = (["cv", "ct", "cs", "cp", "loc", "d_tk", "d_ln", "d_y", "d_x0", "d_x1", "d_t", "d_l"]
              + ["d_il%d" % i for i in range(7)] + ["d_o%d" % i for i in range(8)]
              + ["a%s%d" % (k, n) for k in "zbye" for n in range(ST)])


def rank_program(g, core, T, topo):
    rank = T.rank_of(core)
    if rank is None:
        return
    queues = {"v": g.vector, "t": g.tensor, "s": g.scalar, "p": g, "y": g.sync}
    semof = {"v": "cv", "t": "ct", "s": "cs", "p": "cp"}
    count = {s: 0 for s in SEMAPHORES}
    known = {e: {} for e in queues}
    snaps = {}
    hist = {}

    def conflicts(e, name, lo, hi, write):
        bank = name[0] == "p" and name[1:2].isupper()
        out = []
        for (a, b, e2, s2, v2, w2, asy) in hist.get(name, []):
            if bank:
                if e2 == e:
                    if e == "t" or not (write or w2) or b <= lo or hi <= a:
                        continue
                out.append((s2, v2))
                continue
            if b <= lo or hi <= a or not (write or w2):
                continue
            if e2 == e and not asy and not w2:
                continue
            out.append((s2, v2))
        return out

    def waits(e, acc):
        need = {}
        for (name, lo, hi, w) in acc:
            for s, v in conflicts(e, name, lo, hi, w):
                need[s] = max(need.get(s, 0), v)
        own = semof.get(e)
        for s in sorted(need, key=lambda s: (s == own, s)):
            v = need[s]
            if known[e].get(s, 0) >= v:
                continue
            queues[e].wait_ge(T.sem[s], v)
            for s2, v2 in snaps[(s, v)].items():
                known[e][s2] = max(known[e].get(s2, 0), v2)

    def note(e, acc, s, v, asy):
        sn = dict(known[e]) if e in known else {}
        sn[s] = v
        snaps[(s, v)] = sn
        for (name, lo, hi, w) in acc:
            h = hist.setdefault(name, [])
            if w:
                h[:] = [x for x in h if not (lo <= x[0] and x[1] <= hi)]
            else:
                h[:] = [x for x in h if not (x[2] == e and not x[5] and not asy and lo <= x[0] and x[1] <= hi)]
            h.append((lo, hi, e, s, v, w, asy))

    def access(rd, wr):
        return [(n, lo, hi, False) for (n, lo, hi) in rd] + [(n, lo, hi, True) for (n, lo, hi) in wr]

    def op(e, rd, wr, fn):
        acc = access(rd, wr)
        waits(e, acc)
        s = semof[e]
        count[s] += 1
        fn(queues[e]).then_inc(T.sem[s], 1)
        note(e, acc, s, count[s], False)

    def dma(e, rd, wr, out, in_, s):
        acc = access(rd, wr)
        waits(e, acc)
        count[s] += 16
        queues[e].dma_start(out, in_).then_inc(T.sem[s], 16)
        note(e, acc, s, count[s], True)

    def ap(o):
        if o[0] == "EQ":
            c, a = divmod(o[1], 240)
            return T.EQ[:, c, a:a + o[2] - o[1]] if len(o) == 3 else T.EQ[:, c:o[2] // 240, 0:16]
        if len(o) == 1:
            return T[o[0]][:]
        if len(o) == 4:
            return T[o[0]][:, o[1]:o[2]:o[3]]
        return T[o[0]][:, o[1]:o[2]]

    def rg(o):
        if o[0] == "sa":
            return ("sa%d" % (o[1] % 2), 0, 28)
        return (o[0], 0, SCRATCH[o[0]][1][1]) if len(o) == 1 else (o[0], o[1], o[2])

    def vts(out, i, s1, o0, s2=None, o1=None):
        rd = [rg(i)]
        if isinstance(s1, tuple):
            rd.append(rg(s1))
            s1 = ap(s1)
        if isinstance(s2, tuple):
            rd.append(rg(s2))
            s2 = ap(s2)
        if o1 is None:
            op("v", rd, [rg(out)], lambda q: q.tensor_scalar(ap(out), ap(i), s1, None, o0))
        else:
            op("v", rd, [rg(out)], lambda q: q.tensor_scalar(ap(out), ap(i), s1, s2, o0, o1))

    def vtt(out, a, b, o):
        op("v", [rg(a), rg(b)], [rg(out)], lambda q: q.tensor_tensor(ap(out), ap(a), ap(b), o))

    def vcp(out, i):
        op("v", [rg(i)], [rg(out)], lambda q: q.tensor_copy(ap(out), ap(i)))

    def fill(out, c):
        op("v", [], [rg(out)], lambda q: q.memset(ap(out), c))

    def act(out, i, f, **kw):
        op("s", [rg(i)] + ([("rm", 0, 16)] if "scale" in kw else []), [rg(out)], lambda q: q.activation(ap(out), ap(i), f, **kw))

    def gat(out, win, off):
        op("s", [rg(win), rg(off)], [rg(out)], lambda q: q.activation(ap(out), ap(win).indirect(ap(off)), AF.Copy))

    def mm(out, l, r, start, stop):
        op("t", [rg(l), rg(r)], [rg(out)], lambda q: q.matmul(ap(out), ap(l), ap(r), start, stop))

    def mat(n, r):
        return (n, 128 * r, 128 * r + 128)

    nxt = T.cores[(rank + 1) % NR]
    prv = T.cores[(rank - 1) % NR]
    rid, pid = topo.addr(nxt)[:2]
    emask = topo.mask(core, nxt)
    n_out = len(topo.engines(core, nxt))
    n_in = len(topo.engines(prv, core))

    def send(dst, src, s):
        waits("p", [rg(src) + (False,)])
        g.remote_dma(out_ap=ap(dst), in_ap=ap(src), remote_sem=T.sem[s], local_sem=T.sem["loc"], pid=pid,
                     routing_id=rid, dma_engine_mask=emask)
        count["loc"] += n_out

    def lands(dst, s):
        count[s] = n_in
        note("r", [rg(dst) + (True,)], s, n_in, True)

    def zin(n):
        return ("ZS", 448 * n, 448 * n + 224)

    def ye(n):
        return ("YE", 448 * n, 448 * n + 224)

    def zparts(b, lo, hi):
        return (b, lo, lo + 2 * CH[LATE][0]), (b, lo + 2 * CH[LATE][0], hi)

    def row(n):
        return ("ZS", 448 * n + 224, 448 * n + 448)

    def lst(n, b, lo, hi):
        return (b, 240 * n + lo, 240 * n + hi)

    for n in range(ST):
        lands(("YE", 448 * n, 448 * n + 448), "ay%d" % n)
        lands(lst(n, "EL", 0, 238), "ae%d" % n)
        for z, s in zip(zparts(*zin(n + 1)), "zb"):
            lands(z, "a%s%d" % (s, n))

    fill(("TLi",), 0)
    fill(("ONE",), 1.0)
    for i in range(7):
        b = ("ilb", 512 * i, 512 * i + 512)
        dma("y", [], [rg(b)], ap(b), T.il[:, 512 * i:512 * i + 512], "d_il%d" % i)
    dma("s", [], [("TLi", 0, 224)], T.TLi[0:128:16, 0:224], T.tk0[:], "d_tk")
    dma("s", [], [("TLi", 224, 448)], T.TLi[0:128:16, 224:448], T.ln0[:], "d_ln")
    dma("s", [], [rg(zin(0))], ap(zin(0)), T.y0[:], "d_y")
    for i in range(2):
        b = ("XT", 1792 * i, 1792 * i + 1792)
        dma("y", [], [rg(b)], ap(b), T.xw[:, 1792 * i:1792 * i + 1792], "d_x%d" % i)

    def asel(out, i, pat, cmp, base, cm, other=0.0):
        op("p", [rg(i)], [rg(out)], lambda q: q.affine_select(ap(out), ap(i), pat, cmp, other, base, cm))
    asel(("BO0",), ("ONE",), [[-16, 8], [0, 16]], A.is_ge, 0, 1)
    asel(("ID",), ("ONE",), [[-1, 128]], A.is_equal, 0, 1)
    asel(("BO",), ("BO0",), [[16, 8], [0, 16]], A.is_ge, 15, -1)
    fill(("SEL",), 0.0)
    asel(("SKD",), ("SEL", 0, 1024), [[0, 1024]], A.is_ge, -1, 0)
    asel(mat("BOE", 0), ("BO",), [[0, 8], [-1, 16]], A.is_ge, 7, 0)
    asel(mat("BOE", 1), ("BO",), [[0, 8], [1, 16]], A.is_ge, -8, 0)
    for k, (h, base) in enumerate(((0, 0), (1, 16), (0, -1), (1, 15))):
        asel(mat("P4", k), mat("BOE", h), [[-16, 8], [-2, 16]], A.is_equal, base, 1)
    op("p", [], [("iw", 0, 14)], lambda q: q.iota(T.iw[:], [[16, 14]], 0, 1))
    op("p", [], [("ip", 0, 14)], lambda q: q.iota(T.ip[:], [[0, 14]], 0, 1))
    for r in range(16):
        fill(("th16", r, r + 1), 2.0 * 4.0 ** (15 - r))
    vts(("NID32",), ("ID",), -32.0, A.mult)
    asel(("SKA",), ("SKD",), [[0, 1024]], A.is_ge, -1, 0)
    asel(("ZER",), ("ID",), [[0, 128]], A.is_ge, -1, 0)
    for k in range(2):
        asel(("MASK", 896 * k, 896 * k + 896), ("SKA", 0, 896), [[0, 112], [1, 8]], A.is_equal, 0, 0, 256.0)

    def halves(i):
        lo, hi = 512 * i, 512 * i + 512
        vts(("f16t", lo, hi), ("ilb", lo, hi), -1792.0, A.add)

    def table(i):
        lo, hi = 512 * i, 512 * i + 512
        vts(("LT", lo, hi), ("f16t", lo, hi), 1.0 / 32, A.mult, 184.515625, A.add)
        pb = ("pXR", "pE", "pO", "pZ")[i % 4]
        mm((pb,), ("ID",), ("f16t", lo, hi), True, False)
        mm((pb,), ("NID32",), ("LT", lo, hi), False, True)
        act(("WT", lo, hi), (pb,), AF.Copy, bias=5920.0)

    def clocks():
        vts(("TLj", 0, 224), ("TLi", 0, 224), 4064, A.bitwise_and)
        vts(("TLj", 224, 448), ("TLi", 0, 224), 31, A.bitwise_and)
        vcp(("TLb", 0, 448), ("TLj",))
        vcp(("TLb", 448, 672), ("TLi", 224, 448))
        for r in range(16):
            mm(("pW", 0, 42), mat("SEL", r), ("TLb", r, 672, 16), r == 0, r == 15)

    def places():
        vcp(("c2", 0, 14), ("pW", 14, 28))
        vcp(("bw",), ("pW", 14, 28))
        vts(("b2", 0, 14), ("pW", 28, 42), 32.0, A.mult)
        vcp(("t1",), ("pW", 0, 14))
        vtt(("ao", 0, 14), ("c2", 0, 14), ("b2", 0, 14), A.add)
        vcp(("AO", 0, 14), ("ao", 0, 14))
        vtt(("Tn",), ("t1",), ("c2", 0, 14), A.add)

    def broadcast(dst, src, lo):
        for r in range(16):
            mm((dst, r + lo, lo + 224, 16), mat("BC", r), src, True, True)

    def pick(m, k):
        for h in range(2):
            for t in range(8):
                act((m, 128 * t + 2 * t + h, 128 * t + 128, 16), ("ID", k + 8 * h, 128, 16), AF.Copy)

    def weights():
        op("p", [], [("trm", 0, 224)], lambda q: q.iota(T.trm[:], [[1, 224]], NP, 0, allow_small_or_imprecise_dtypes=True))
        vtt(("rq",), ("rm",), ("th16",), A.mult)
        vcp(("DG", 0, 16), ("rm",))
        vts(("ipq",), ("ip",), 112, A.bitwise_and)
        vts(("BIG",), ("BO",), 2.0 ** 32, A.mult)
        op("v", [("rq", 0, 16)], [("wq1", 0, 1)], lambda q: q.tensor_reduce(T.wq1[:], T.rq[:], AxisListType.X, A.add))
        vcp(("DG", 16, 32), ("DG", 0, 16))
        vtt(("iw",), ("iw",), ("ipq",), A.subtract)
        fill(("sd",), 0.0)
        fill(("Ar",), 0.0)
        vcp(("DG", 32, 64), ("DG", 0, 32))
        vts(("WQ",), ("BO",), ("wq1", 0, 1), A.mult, 0.5, A.mult)
        vts(("b2", 14, 28), ("iw",), 16.0, A.mult)
        vcp(("DG", 64, 128), ("DG", 0, 64))
        vts(("NID",), ("ID",), -1.0, A.mult)
        vcp(("DG", 128, 224), ("DG", 0, 96))
        vts(("thA",), ("DG",), ("wq1", 0, 1), A.mult)
        vts(("thB",), ("DG",), 1.0, A.subtract)

    for r in range(16):
        act(("SEL", 128 * r + r, 128 * r + 128, 16), ("BO", r, 128, 16), AF.Copy)
    halves(0)
    vtt(("h64",), ("ID", 0, 64), ("ID", 64, 128), A.add)
    halves(1)
    vtt(("h32",), ("h64", 0, 32), ("h64", 32, 64), A.add)
    table(0)
    vtt(("rm",), ("h32", 0, 16), ("h32", 16, 32), A.add)
    halves(2)
    for r in range(16):
        act(mat("BC", r), ("BO",), AF.Copy, scale=T.rm[:, r:r + 1])
    table(1)
    halves(3)
    table(2)
    halves(4)
    table(3)
    halves(5)
    table(4)
    clocks()
    halves(6)
    table(5)
    pick("SKD", 7)
    table(6)
    places()
    broadcast("pS", ("bw",), 256)
    act(row(0), ("pS", 256, 480), AF.Copy)
    vts(("PM32",), ("P4",), -32.0, A.mult)
    vts(("P32",), ("P4",), 32.0, A.mult)
    weights()

    def reduced(i, k):
        lo, hi = 512 * i, 512 * i + 512
        if k == 0:
            vts(("KF", lo, hi), ("WT", lo, hi), 1.0 / 32, A.mult, 191.515625, A.add)
        elif k == 1:
            pb = ("pE", "pO", "pZ")[i % 3]
            mm((pb,), ("ID",), ("WT", lo, hi), True, False)
            mm((pb,), ("NID32",), ("KF", lo, hi), False, True)
            act(("YW", lo, hi), (pb,), AF.Copy, bias=6144.0)
        elif k == 2:
            vts(("f16t", lo, hi), ("KF", lo, hi), -32.0, A.mult, 6144.0, A.add)
        else:
            vtt(("YW", lo, hi), ("WT", lo, hi), ("f16t", lo, hi), A.add)
        if k % 2:
            dma("y", [("YW", lo, hi)], [], T.yw[:, lo:hi], T.YW[:, lo:hi], "d_o%d" % (1 + i))

    def more(n, i):
        if n == ST:
            reduced(i, 0)
            reduced(i, 1)

    def arrive(n):
        z = zin(n)
        vtt(("ZS", 448 * n + 224, 448 * n + 448), z, ("pD", 256, 480), A.is_ge)
        for r in range(16):
            mm(("pW", 0, 28), mat("SEL", r), ("ZS", 448 * n + r, 448 * n + 448, 16), r == 0, r == 15)
        vtt(("o2",), ("SC", 15, 224, 16), ("DW",), A.max)
        vts(("SI",), ("pS", 0, 28), 1792.0, A.add)
        vcp(("OFF", 0, 14), ("o2",))
        vts(("SJ",), ("SI",), 4064, A.bitwise_and)
        op("v", [rg(z), ("DRED", 0, 224), ("OFF", 0, 14)], [("WT", 0, NP + NB)],
           lambda q: q.tensor_tensor(T.WT[:, 0:NP + NB].indirect(T.OFF[:, 0:14]), T.DRED[:], ap(z), A.add))
        more(n, 0)
        more(n, 1)
        vtt(("sd", 1, 28, 2), ("SJ", 14, 28), ("SJ", 0, 14), A.subtract)
        vcp(("sa", 1, 28, 2), ("SJ", 0, 14))
        vts(("sa", 0, 28, 2), ("pW", 14, 28), 9.0, A.is_ge)
        if n < ST:
            vtt(("q",), ("pW", 0, 14), ("B1",), A.add)
        vcp(("t1",), ("pW", 0, 14))
        more(n, 2)
        op("v", [("sd", 0, 28), ("sa0", 0, 28), ("sa1", 0, 28)], [("lin", 0, 28)],
           lambda q: q.tensor_tensor_scan(T.lin[:], T.sd[:], T.sa[:], 0.0, A.mult, A.add))
        if n < ST:
            vts(("c2", 0, 14), ("q",), 31, A.bitwise_and)
            vts(("c2", 14, 28), ("q",), 15, A.bitwise_and)
        vts(("t2",), ("t1",), 31, A.bitwise_and)
        if n < ST:
            vtt(("ao", 0, 14), ("c2", 0, 14), ("lin", 1, 28, 2), A.add)
            vtt(("ao", 14, 28), ("c2", 14, 28), ("b2", 14, 28), A.add)
        more(n, 3)
        vtt(("t3",), ("t2",), ("B1",), A.add)
        if n < ST:
            vcp(("AO", 0, 14), ("ao", 0, 14))
            vcp(("AO", 14, 28), ("ao", 14, 28))
            vcp(("bw",), ("c2", 0, 14))
            vcp(("sel",), ("sa", 0, 28, 2))
        more(n, 4)
        vts(("Tn",), ("t3",), 4095, A.bitwise_and)
        if n < ST:
            op("v", [rg(z), ("AO", 14, 28)], [("XT", 0, NP)],
               lambda q: q.tensor_copy(T.XT[:, 0:NP].indirect(T.AO[:, 14:28]), ap(z)))

    def fetch(n):
        parts = ((0, CUT, "pXR", ("pE", "pO")), (CUT, NB, "pC", ("pD", "pS")))
        br = ("BR", 0) if n else row(0)[:2]

        def x(o, lo, hi, h=None):
            return (o[0], o[1] + lo, o[1] + hi) if h is None else (o[0], o[1] + lo + h, o[1] + hi, 2)

        def lists(part, src, k):
            lo, hi, _, banks = parts[part]
            for h in range(2):
                mm((banks[k // 2], lo // 2, hi // 2), mat({"WA": "P4", "LG": "P32", "KQ": "PM32"}[src], k + h),
                   x((src, 0), lo, hi, h), False, src == "KQ" and h == 1)

        def floors(part):
            lo, hi, b, _ = parts[part]
            mm((b, lo, hi), ("ID",), ("WA", lo, hi), False, True)
            vts(("KQ", lo, hi), (b, lo, hi), 1.0 / 32, A.mult, 1535.515625, A.add)

        for lo, hi, b, banks in parts:
            gat(("WA", lo, hi), ("WT", 0, NP), ("AO", lo // 16, hi // 16))
            gat(("LG", lo, hi), ("LT", 0, NP), ("AO", lo // 16, hi // 16))
            mm((b, lo, hi), ("ID",), x(br, lo, hi), True, False)
            if n:
                mm((b, lo, hi), ("BO",), x(zin(n), lo, hi), False, False)
        for lo, hi, b, banks in parts:
            for k in (0, 2):
                for h in range(2):
                    mm((banks[k // 2], lo // 2, hi // 2), mat("P4", k + h), x(br, lo, hi, h), h == 0, False)
                for h in range(2 if n else 0):
                    mm((banks[k // 2], lo // 2, hi // 2), mat("BOE", h), x(zin(n), lo, hi, h), False, False)
        floors(0)
        vts(lst(n, "EF", 224, 238), ("Tn",), -2048.0, A.add)
        lists(0, "WA", 0)
        lists(0, "LG", 0)
        lists(0, "WA", 2)
        floors(1)
        for src, k in (("KQ", 0), ("LG", 2), ("KQ", 2)):
            lists(0, src, k)
        for src, k in (("WA", 0), ("LG", 0), ("KQ", 0), ("WA", 2), ("LG", 2), ("KQ", 2)):
            lists(1, src, k)
        for lo, hi, _, banks in parts:
            for b, o in ((banks[0], 0), (banks[1], 112)):
                vts(lst(n, "EO", o + lo // 2, o + hi // 2), (b, lo // 2, hi // 2), 45024.0, A.add)
                vts(lst(n, "EF", o + lo // 2, o + hi // 2), (b, lo // 2, hi // 2), 43232.0, A.add)

    def big(n):
        for (a, b) in CH:
            gat(("VE", 16 * a, 16 * b), ("XT", 0, NP), lst(n, "EO", a, b))
            if n and b == CH[RB][1]:
                broadcast("pS", ("bw",), 256)
                act(row(n), ("pS", 256, 480), AF.Copy)
        last = 2 * CH[LATE][0]
        early, late = zparts(*zin(n))
        mm(("pZ", 0, last), ("NID",), early, True, False)
        mm(("pC", 256 + last, 480), ("NID",), late, True, False)

        def least(a, b):
            off = lst(n, "EO", 112 + a, 112 + b)
            op("v", [("XT", 0, NP), rg(off), ("VE", 16 * a, 16 * b)], [("U", 16 * a, 16 * b)],
               lambda q: q.tensor_tensor(T.U[:, 16 * a:16 * b], T.XT[:, 0:NP].indirect(ap(off)), T.VE[:, 16 * a:16 * b], A.min))

        def greatest(a, b):
            r = slice(16 * a, 16 * b)
            op("v", [("MASK", 16 * a, 16 * b), ("U", 16 * a, 16 * b)], [("M", 16 * a, 16 * b)],
               lambda q: q.tensor_tensor_scan(T.M[:, r], T.MASK[:, r], T.U[:, r], 0.0, A.min, A.max))
            o = ("pZ", 2 * a, 2 * b) if 2 * b <= last else ("pC", 256 + 2 * a, 256 + 2 * b)
            mm(o, ("ID",), ("M", 16 * a + 7, 16 * b, 8), False, 2 * b in (last, 224))
        for i, c in enumerate(CH):
            least(*c)
            if i:
                greatest(*CH[i - 1])
        if n:
            op("v", [("pW", 32, 46)], [("Ar", 0, 1)], lambda q: q.tensor_reduce(T.Ar[:], T.pW[:, 32:46], AxisListType.X, A.add))
        greatest(*CH[-1])
        out = zparts("ZO", 224 * n, 224 * n + 224)
        act(out[0], ("pZ", 0, last), AF.Abs)
        act(out[1], ("pC", 256 + last, 480), AF.Abs)
        send(("YE", 448 * n, 448 * n + 448), ("ZS", 448 * n, 448 * n + 448), "ay%d" % n)
        for d, o, s in zip(zparts(*zin(n + 1)), out, "zb"):
            send(d, o, "a%s%d" % (s, n))

    def ready(n):
        el = 240 * n
        for k in (7, 15):
            mm(("pD", k // 8, 224, 2), mat("BC", k), ("EL", el + 112, el + 224), True, True)
        for t in range(8):
            mm(("pS", 32, 46), mat("SKD", t), ("EL", el + 112 + t, el + 224, 8), t == 0, t == 7)
        if n == 0:
            pick("SKA", 0)
            vtt(("trm",), ("trm",), ("DG",), A.mult)
            vtt(("thr",), ("thA",), ("thB",), A.add)
        vts(("KA",), ("Ar",), 1.0 / 32, A.mult, 191.515625, A.add)
        vts(("Au",), ("KA",), -32.0, A.mult, 6145.0, A.add)
        vts(("DR",), ("pD", 0, 224), 1792.0, A.add)
        vts(("DW",), ("pS", 32, 46), 1792.0, A.add)
        vts(("A1",), ("Au",), ("Ar", 0, 1), A.add)
        vcp(("DWu", 0, 14), ("DW",))
        gat(("DO",), ("WT", 0, NP), ("DWu", 0, 14))
        half = (("pC", 0, 112), ("pE", 112, 224))
        for b, lo, hi in half:
            mm((b, lo, hi), ("ZER",), ("MASK", lo, hi), True, False)

        def strips(h):
            mm(half[h], ("WQ",), ("EQ", 7 * 240 * h, 7 * 240 * (h + 1), 1), False, True)

        def losers(h):
            b, lo, hi = half[h]
            vtt(("LF", lo, hi), (b, lo, hi), ("thr", lo, hi), A.is_gt)
            op("v", [("trm", lo, hi), ("LF", lo, hi)], [("SC", lo, hi)],
               lambda q: q.tensor_tensor_scan(T.SC[:, lo:hi], T.trm[:, lo:hi], T.LF[:, lo:hi], 0.0, A.max, A.mult))

        for c in range(14):
            e = ("EQ", 240 * c, 240 * c + 224 - 16 * c)
            vts(e, ("DR", 16 * c, 224), ("DW", c, c + 1), A.is_equal)
            for b, lo, hi in half:
                lo = max(lo, 16 * c + 16)
                if lo < hi:
                    mm((b, lo, hi), ("BIG",), (e[0], e[1] + lo - 16 * c, e[1] + hi - 16 * c), False, False)
            if c % 7 == 6:
                strips(c // 7)
            if c == 2:
                vts(("B1",), lst(n, "EL", 224, 238), ("A1", 0, 1), A.add, 2048.0, A.add)
            if c == 9:
                vts(("KD",), ("DO",), 1.0 / 32, A.mult, 191.515625, A.add)
        losers(0)
        losers(1)
        mm(("pZ", 0, 224), ("ID",), ("DO",), True, False)
        mm(("pZ", 0, 224), ("NID32",), ("KD",), False, True)
        act(("DRED",), ("pZ", 0, 224), AF.Copy, bias=5984.0)
        mm(("pD", 256, 480), ("ID",), ye(n), True, True)
        for t in range(8):
            mm(("pS", 0, 28), mat("SKA", t), ("EL", el + t, el + 224, 8), t == 0, t == 7)
        if n < ST - 1:
            op("s", [(ye(n)[0], ye(n)[2], ye(n)[2] + 224), ("A1", 0, 1)], [("BR", 0, 224)],
               lambda q: q.activation(T.BR[:], T.YE[:, 448 * n + 224:448 * n + 448], AF.Identity, bias=T.A1[:]))

    for n in range(ST):
        if n:
            arrive(n)
        fetch(n)
        if n:
            mm(("pW", 32, 46), ("ONE",), ("sel",), True, True)
        send(lst(n, "EL", 0, 238), lst(n, "EF", 0, 238), "ae%d" % n)
        big(n)
        ready(n)

    dma("y", [rg(zin(ST))], [], T.yy[:], ap(zin(ST)), "d_o0")
    arrive(ST)
    vts(("fo", 0, 14), ("Tn",), -2048.0, A.add)
    vcp(("fo", 14, 28), ("lin", 1, 28, 2))
    for r in range(16):
        mm(("pS", r, 448, 16), mat("BC", r), ("fo",), True, True)
    for i, k in ((5, 0), (6, 0), (5, 2), (6, 2), (5, 3), (6, 3)):
        reduced(i, k)
    vts(("fr", 0, 224), ("pS", 0, 224), 2048.0, A.add)
    vts(("fr", 224, 448), ("pS", 224, 448), 1.0 / 32, A.mult)
    dma("s", [("fr", 0, 224)], [], T.yt[:], T.fr[0:128:16, 0:224], "d_t")
    dma("s", [("fr", 224, 448)], [], T.yl[:], T.fr[0:128:16, 224:448], "d_l")
    for s in SEMAPHORES:
        if count[s] and known["p"].get(s, 0) < count[s]:
            g.wait_ge(T.sem[s], count[s])
